import numpy as np, ml_dtypes
CORES = [3,7,11,15,131,135,139,143]
N = 8
import mx_ref
BF = ml_dtypes.bfloat16
def entries(a):
    return np.ascontiguousarray(a.T).reshape(-1)
def table(e):
    return np.ascontiguousarray(np.reshape(e, (-1, 16)).T).astype(np.int32)
def cut(t, i, w=512):
    return t[:, w * i:w * i + w]
def f(rng, *shape):
    return mx_ref.flush((rng.standard_normal(shape, dtype=np.float32) * np.exp2(rng.integers(-2, 3, shape[:-1] + (1,)))).astype(BF))
def wide(rng, *shape, cols=0):
    v = rng.standard_normal(shape, dtype=np.float32) * np.exp2(rng.integers(-12, 13, shape)).astype(np.float32)
    if cols: v *= np.repeat(np.exp2(rng.integers(-cols, cols + 1, shape[:-2] + (1, shape[-1] // 4))) * (rng.random(shape[:-2] + (1, shape[-1] // 4)) > 0.0625), 4, axis=-1).astype(np.float32)
    return mx_ref.flush(v.astype(BF))
PG, NW, SP, CW, CP, O = 16, 64, 16, 16, 4, 2
def counts(rng, total, cap, least):
    n = np.array(least)
    while n.sum() < total: n[rng.choice(np.flatnonzero(n < cap))] += 1
    return n
def lists(rng, full=False, own=False, shared=False, rewritten=False):
    h = int(rng.integers(0, N)); hot = rng.permutation(PG)[:CP if shared else 2]
    fr, pg = np.zeros((N, SP), int), np.zeros((N, SP), int)
    rd, wr, wp = np.full((N, N * CP), -1), np.full((N, N * CW), -1), np.full((N, N * CW), -1)
    for s in range(N):
        lw, lp = np.zeros(N, int), np.zeros(N, int)
        if full:
            a = np.append(h, rng.permutation(np.delete(np.arange(N), h)))
            lw[a[:NW // CW]] = CW; lp[a[:SP // CP]] = CP
        if own: lw[s] = CW; lp[s] = CP
        if shared: lw[h] = CW; lp[h] = CP
        if rewritten: lw[h] = CW; lp[h] = 1
        n, fresh, at = counts(rng, NW, CW, lw), rng.permutation(NW), 0
        for q in range(N):
            c = rng.permutation(CW)[:n[q]]
            wr[s, q * CW + c] = fresh[at:at + n[q]]; wp[q, s * CW + c] = 0; at += n[q]
        n, slots, frames = counts(rng, SP, CP, lp), [], []
        for q in range(N):
            must = np.zeros(0, int)
            if q == h and shared: must = hot
            if q == h and rewritten: must = hot[s % 2:s % 2 + 1]
            g = np.concatenate([must, rng.permutation(np.setdiff1d(np.arange(PG), must))])[:n[q]]
            c = rng.permutation(CP)[:n[q]]
            rd[q, s * CP + c] = g; slots.append(q * CP + c); frames.append(q * PG + g)
        o = rng.permutation(SP)
        pg[s] = np.concatenate(slots)[o]; fr[s] = np.concatenate(frames)[o]
    for q in range(N):
        k = np.flatnonzero(wp[q] >= 0); must = np.zeros(0, int)
        if q == h and shared: must = 16 * hot + rng.integers(0, 16, hot.size)
        if q == h and rewritten: must = (16 * hot[:, None] + np.arange(16)).reshape(-1)
        p = np.concatenate([must, rng.permutation(np.setdiff1d(np.arange(16 * PG), must))])[:k.size]
        wp[q, k] = rng.permutation(p)
    return {n: np.stack([table(v) for v in a]) for n, a in (("fr", fr), ("wr", wr), ("wp", wp), ("rd", rd), ("pg", pg))}
def setup_inputs(rng):
    return {"pl": f(rng, N, 128, 64 * PG), "nw": f(rng, N, 128, 4 * NW), "qw": f(rng, N, 128, 512 * O), **lists(rng)}
def setup_inputs_full(rng):
    return {**setup_inputs(rng), **lists(rng, full=True)}
def setup_inputs_own(rng):
    return {**setup_inputs(rng), **lists(rng, own=True)}
def setup_inputs_rewritten(rng):
    return {**setup_inputs(rng), **lists(rng, rewritten=True)}
def setup_inputs_shared(rng):
    return {**setup_inputs(rng), **lists(rng, shared=True)}
def setup_inputs_spread(rng):
    d = setup_inputs(rng); d["pl"] = wide(rng, N, 128, 64 * PG, cols=8); d["nw"] = wide(rng, N, 128, 4 * NW, cols=8); return d
def check_inputs(d):
    b = []
    for r in range(N):
        t, a, p, k, g = [entries(d[n][r]) for n in ("fr", "wr", "wp", "rd", "pg")]
        if t.min() < 0 or t.max() >= N * PG or len(set(t.tolist())) != SP: b.append("fr")
        if a.min() < -1 or a.max() >= NW or sorted(a[a >= 0].tolist()) != list(range(NW)): b.append("wr")
        sent = np.concatenate([entries(d["wr"][s])[r * CW:r * CW + CW] for s in range(N)]); v = p[p >= 0]
        if p.min() < -1 or p.max() >= 16 * PG or len(set(v.tolist())) != v.size or ((p >= 0) != (sent >= 0)).any(): b.append("wp")
        if k.min() < -1 or k.max() >= PG: b.append("rd")
        got = np.concatenate([entries(d["rd"][q])[r * CP:r * CP + CP] for q in range(N)])
        if g.min() < 0 or g.max() >= N * CP or len(set(g.tolist())) != SP or (got >= 0).sum() != SP: b.append("pg")
        elif (got[g] < 0).any() or (g // CP * PG + got[g] != t).any(): b.append("pg")
    return b
def reference(pl, nw, qw, fr, wr, wp, rd, pg):
    pools = []
    for q in range(N):
        v = pl[q].reshape(128, 16 * PG, 4).copy()
        for s in range(N):
            c, p = entries(wr[s])[q * CW:q * CW + CW], entries(wp[q])[s * CW:s * CW + CW]
            k = p >= 0
            v[:, p[k]] = nw[s].reshape(128, NW, 4)[:, c[k]]
        pools.append(v)
    pools = np.concatenate(pools, axis=1)
    y = np.zeros((N, 128, O * SP * 16), np.float32)
    for r in range(N):
        e = (16 * entries(fr[r])[:, None] + np.arange(16)).reshape(-1)
        pages = mx_ref.quantize(np.ascontiguousarray(pools[:, e]).reshape(128, -1))
        for o in range(O):
            y[r][:, SP * 16 * o:SP * 16 * o + SP * 16] = mx_ref.matmul(mx_ref.quantize(np.ascontiguousarray(cut(qw[r], o))), pages)
    return {"y": y}

@@ -1,0 +1,260 @@
+from concourse.bass import DstId, RemoteDMATransfer
+from concourse.mybir import dt, AluOpType, ActivationFunctionType
+
+N, PG, NW, SP, CW, CP, O = 8, 16, 64, 16, 16, 4, 2
+POOL = 16 * PG
+PAGE = 16 * CP
+OWN = POOL + N * CW
+WIDE = OWN + 2 * CW
+F8 = "float8_e4m3fn_x4"
+
+SCRATCH = {
+    "nwt": ("sbuf", [128, 512], "bfloat16"),
+    "plt": ("sbuf", [128, 4 * POOL], "bfloat16"),
+    "qwt": ("sbuf", [128, 512 * O], "bfloat16"),
+    "nwq": ("sbuf", [128, 128], F8), "nws": ("sbuf", [128, 128], "uint8"),
+    "qwq": ("sbuf", [128, 128 * O], F8), "qws": ("sbuf", [128, 128 * O], "uint8"),
+    "slot1": ("sbuf", [128, N * CW], F8), "slot1s": ("sbuf", [128, N * CW], "uint8"),
+    "win": ("sbuf", [128, WIDE], F8), "wins": ("sbuf", [128, WIDE], "uint8"),
+    "slot2": ("sbuf", [128, N * PAGE], F8), "slot2s": ("sbuf", [128, N * PAGE], "uint8"),
+    "land2": ("sbuf", [128, N * PAGE], F8), "land2s": ("sbuf", [128, N * PAGE], "uint8"),
+    "fin": ("sbuf", [128, POOL], F8), "fins": ("sbuf", [128, POOL], "uint8"),
+    "wrt": ("sbuf", [32, N * CW // 16], "int32"),
+    "wpt": ("sbuf", [32, N * CW // 16], "int32"),
+    "rdt": ("sbuf", [32, N * CP // 16], "int32"),
+    "pgrow": ("sbuf", [1, SP], "int32"), "pgb": ("sbuf", [128, SP], "int32"),
+    "cval": ("sbuf", [128, N * CW], "float32"),
+    "cdmp": ("sbuf", [128, N * CW // 16], "int32"),
+    "ccol": ("sbuf", [128, POOL], "float32"), "coff": ("sbuf", [128, POOL], "float32"),
+    "cmask": ("sbuf", [128, POOL], "float32"), "cnot": ("sbuf", [128, POOL], "float32"),
+    "crow": ("sbuf", [128, 1], "int32"), "crow16": ("sbuf", [128, 1], "int32"),
+    "crowp": ("sbuf", [128, 1], "float32"), "crowf": ("sbuf", [128, 1], "float32"), "crown": ("sbuf", [128, 1], "float32"),
+    "wpa": ("sbuf", [32, N * CW // 16], "int32"), "wpb": ("sbuf", [32, N * CW // 16], "int32"),
+    "comp": ("sbuf", [128, 512], "float32"),
+    "mine": ("sbuf", [128, POOL], "float32"), "last": ("sbuf", [128, POOL], "float32"),
+    "offw": ("sbuf", [128, N * CW // 16], "uint16"),
+    "offp": ("sbuf", [128, N * CW // 16], "uint16"), "offr": ("sbuf", [128, N * CP // 16], "uint16"),
+    "list2": ("sbuf", [128, N * CP], "uint16"), "off3": ("sbuf", [128, SP], "uint16"),
+    "acc": ("psum", [128, 512 * 4], "float32"),
+    "yt": ("sbuf", [128, 256 * O], "float32"),
+}
+DMA_SEMS = ["d_nw", "d_wr", "d_pl", "d_wp", "d_rd", "d_pg", "d_qw", "d_y"]
+EVENTS = ["zero", "offw", "q_nw", "c1", "s1", "own_c", "own_s", "q_pl", "q_qw",
+          "i_comp", "i_col", "i_row", "k_val", "k_dmp", "k_coff", "k_mask", "k_not", "k_row", "k_rowp", "k_rowf", "k_rown",
+          "k_wpa", "k_wpb", "k_offp", "k_comp", "k_mine", "k_last", "k_offr", "k_list2", "pgb", "k_off3",
+          "c2_0", "c2_1", "s2_0", "s2_1", "own2_c", "own2_s", "fc0", "fc1", "fs0", "fs1",
+          "m00", "m01", "m10", "m11", "y0", "y1"]
+SEMAPHORES = DMA_SEMS + EVENTS + ["in_c1", "in_s1", "in_c2", "in_s2", "sent"]
+
+
+def kinds(src, cores, topo):
+    peer = [d for d in cores if d != src and d in topo.cores_of(src)]
+    off = [d for d in cores if d not in topo.cores_of(src)]
+    near = [d for d in off if topo.mates(src, d)] + [d for d in off if topo.same_plane(src, d)]
+    return near, [d for d in off if d not in near], peer
+
+
+def plan(src, cores, topo):
+    near, far, peer = kinds(src, cores, topo)
+    e = topo.engines(src, near[0])
+    a, b = e[0::2], e[1::2]
+    out = {}
+    for i, d in enumerate(near):
+        out[d] = ([a[i]], [b[i]], e[2 * i:2 * i + 2])
+    for i, d in enumerate(far):
+        out[d] = (b[2 * i:2 * i + 2], a[2 * i:2 * i + 2], e[4 * i:4 * i + 4])
+    for d in peer:
+        rest = [x for x in topo.engines(src, d) if x not in e]
+        out[d] = ([rest[0]], [rest[2]], [rest[0], rest[2]])
+    return out
+
+
+def runs(ranks):
+    out = []
+    for r in sorted(ranks):
+        if out and out[-1][1] == r:
+            out[-1] = (out[-1][0], r + 1)
+        else:
+            out.append((r, r + 1))
+    return out
+
+
+def rank_program(g, core, T, topo):
+    rank = T.rank_of(core)
+    if rank is None:
+        return
+    sem = T.sem
+    v, s, y, t = g.vector, g.scalar, g.sync, g.tensor
+    fn = ActivationFunctionType
+    copy = fn.Copy
+    cores = list(T.cores)
+    near, far, peer = kinds(core, cores, topo)
+    ways = plan(core, cores, topo)
+    came = [plan(d, cores, topo)[core] for d in cores if d != core]
+    arrivals = [sum(len(w[k]) for w in came) for k in range(3)]
+
+    def wait(q, *names):
+        for n in names:
+            q.wait_ge(sem[n], 1)
+
+    def codes(view):
+        return view.bitcast(dt.uint32)
+
+    y.dma_start(T.nwt[:, 0:4 * NW], T.nw[:]).then_inc(sem.d_nw, 16)
+    for k in range(2):
+        s.dma_start(T.wrt[16 * k:16 * k + 16, :], T.wr[:]).then_inc(sem.d_wr, 16)
+    s.dma_start(T.plt[:], T.pl[:]).then_inc(sem.d_pl, 16)
+    for k in range(2):
+        y.dma_start(T.wpt[16 * k:16 * k + 16, :], T.wp[:]).then_inc(sem.d_wp, 16)
+    for k in range(2):
+        y.dma_start(T.rdt[16 * k:16 * k + 16, :], T.rd[:]).then_inc(sem.d_rd, 16)
+    y.dma_start(T.pgrow[0:1, :], T.pg[:]).then_inc(sem.d_pg, 16)
+    y.dma_start(T.qwt[:], T.qw[:]).then_inc(sem.d_qw, 16)
+
+    fl = dict(allow_small_or_imprecise_dtypes=True)
+    g.iota(T.crow[:], [[0, 1]], 0, 1).then_inc(sem.i_row, 1)
+    g.iota(T.comp[:, 0:POOL], [[1, POOL]], 0, 0, **fl).then_inc(sem.i_comp, 1)
+    g.iota(T.ccol[:], [[0, 16], [1, 16]], 0, 0, **fl).then_inc(sem.i_col, 1)
+    v.memset(T.nwt[:, 4 * NW:512], 0.0).then_inc(sem.zero, 1)
+    wait(v, "i_row")
+    v.tensor_scalar(T.crow16[:], T.crow[:], 15, None, AluOpType.bitwise_and).then_inc(sem.k_row, 1)
+    v.tensor_copy(T.crowp[:], T.crow[:]).then_inc(sem.k_rowp, 1)
+    wait(v, "k_row")
+    v.tensor_copy(T.crowf[:], T.crow16[:]).then_inc(sem.k_rowf, 1)
+    wait(v, "k_rowf")
+    v.tensor_scalar(T.crown[:], T.crowf[:], -1.0, None, AluOpType.mult).then_inc(sem.k_rown, 1)
+    wait(v, "i_comp", "k_rowp")
+    odd = CW * (rank % 2)
+    pieces = [p for p in ((0, CW * rank, POOL), (CW * rank, CW * rank + CW, OWN + odd - CW * rank), (CW * rank + CW, N * CW, POOL)) if p[0] < p[1]]
+    for a, b, add in pieces:
+        v.tensor_scalar(T.cval[:, a:b], T.comp[:, a:b], float(add), None, AluOpType.add).then_inc(sem.k_val, 1)
+    v.tensor_scalar(T.cdmp[:], T.comp[:, 0:N * CW:16], T.crowp[:, 0:1], float(POOL), AluOpType.add, AluOpType.add).then_inc(sem.k_dmp, 1)
+
+    v.wait_ge(sem.d_wr, 32)
+    for k in range(4):
+        v.tensor_copy(T.offw[32 * k:32 * k + 32, :], T.wrt[:]).then_inc(sem.offw, 1)
+    v.wait_ge(sem.d_nw, 16)
+    wait(v, "zero")
+    v.quantize_mx(T.nwq[:], T.nws[:], T.nwt[:]).then_inc(sem.q_nw, 1)
+    v.wait_ge(sem.offw, 4)
+    wait(v, "q_nw")
+    v.tensor_copy(codes(T.slot1[:, 0:N * CW]), codes(T.nwq[:, 0:NW]).indirect(T.offw[:, 0:8])).then_inc(sem.c1, 1)
+    s.wait_ge(sem.offw, 4)
+    wait(s, "q_nw")
+    s.activation(T.slot1s[:, 0:N * CW], T.nws[:, 0:NW].indirect(T.offw[:, 0:8]), copy).then_inc(sem.s1, 1)
+
+    def send(dests, src, dst, width, base, part, bits, arrive):
+        tr = []
+        for d in dests:
+            q = T.rank_of(d)
+            rid, pid = topo.addr(d, core)
+            a, b = src[:, width * q:width * q + width], dst[:, base + width * rank:base + width * rank + width]
+            if bits:
+                a, b = a.bitcast(dt.uint8), b.bitcast(dt.uint8)
+            tr.append(RemoteDMATransfer(dst_ids=[DstId(rid=rid, pnc=pid)], dma_engine_mask=sum(1 << e for e in ways[d][part]),
+                                        remote_sem=sem[arrive], src=a, dst=b))
+        g.remote_dma_fused(tr, local_sem=sem.sent)
+        return sum(len(ways[d][part]) for d in dests)
+
+    sent = 0
+    wait(g, "c1")
+    sent += send(far + near + peer, T.slot1, T.win, CW, POOL, 0, True, "in_c1")
+    wait(g, "s1")
+    sent += send(far + near + peer, T.slot1s, T.wins, CW, POOL, 1, False, "in_s1")
+
+    lst = T.offw[:, rank - rank % 2:rank - rank % 2 + 2]
+    v.tensor_copy(codes(T.win[:, OWN:WIDE]), codes(T.nwq[:, 0:NW]).indirect(lst)).then_inc(sem.own_c, 1)
+    s.activation(T.wins[:, OWN:WIDE], T.nws[:, 0:NW].indirect(lst), copy).then_inc(sem.own_s, 1)
+
+    wait(s, "i_col", "k_rown")
+    s.activation(T.coff[:], T.ccol[:], fn.Square, bias=T.crown[:, 0:1]).then_inc(sem.k_coff, 1)
+    wait(s, "k_coff")
+    s.activation(T.cmask[:], T.coff[:], fn.Relu, bias=1.0, scale=-1.0).then_inc(sem.k_mask, 1)
+    s.activation(T.cnot[:], T.coff[:], fn.Sign).then_inc(sem.k_not, 1)
+    v.wait_ge(sem.d_wp, 32)
+    v.tensor_scalar(T.wpa[:], T.wpt[:], 4095, None, AluOpType.bitwise_and).then_inc(sem.k_wpa, 1)
+    wait(v, "k_wpa", "k_dmp")
+    v.tensor_tensor(T.wpb[:], T.wpa[:], T.cdmp[0:32, :], AluOpType.min).then_inc(sem.k_wpb, 1)
+    wait(v, "k_wpb")
+    for k in range(4):
+        v.tensor_copy(T.offp[32 * k:32 * k + 32, :], T.wpb[:]).then_inc(sem.k_offp, 1)
+    v.wait_ge(sem.k_val, len(pieces))
+    v.wait_ge(sem.k_offp, 4)
+    v.tensor_copy(T.comp[:, 0:512].indirect(T.offp[:, 0:8]), T.cval[:]).then_inc(sem.k_comp, 1)
+    v.wait_ge(sem.d_rd, 32)
+    for k in range(4):
+        v.tensor_scalar(T.offr[32 * k:32 * k + 32, :], T.rdt[:], 16, 15, AluOpType.mult, AluOpType.add).then_inc(sem.k_offr, 1)
+    wait(v, "k_mask", "k_comp")
+    v.tensor_tensor(T.mine[:], T.comp[:, 0:POOL], T.cmask[:], AluOpType.mult).then_inc(sem.k_mine, 1)
+    wait(v, "k_mine", "k_not")
+    v.tensor_tensor_scan(T.last[:], T.cnot[:], T.mine[:], 0.0, AluOpType.mult, AluOpType.add).then_inc(sem.k_last, 1)
+    wait(v, "k_last")
+    v.wait_ge(sem.k_offr, 4)
+    v.tensor_copy(T.list2[:], T.last[:, 0:POOL].indirect(T.offr[:, 0:2])).then_inc(sem.k_list2, 1)
+    v.wait_ge(sem.d_pl, 16)
+    v.quantize_mx(T.win[:, 0:POOL], T.wins[:, 0:POOL], T.plt[:]).then_inc(sem.q_pl, 1)
+
+    groups = [far, near + peer]
+    picks = [runs([T.rank_of(d) for d in ds]) for ds in groups]
+    wait(v, "k_list2", "q_pl", "own_c")
+    v.wait_ge(sem.in_c1, arrivals[0])
+    wait(s, "k_list2", "q_pl", "own_s")
+    s.wait_ge(sem.in_s1, arrivals[1])
+    for k in range(2):
+        for a, b in picks[k]:
+            lst = T.list2[:, CP * a:CP * b]
+            v.tensor_copy(codes(T.slot2[:, PAGE * a:PAGE * b]), codes(T.win[:, 0:WIDE]).indirect(lst)).then_inc(sem["c2_%d" % k], 1)
+            s.activation(T.slot2s[:, PAGE * a:PAGE * b], T.wins[:, 0:WIDE].indirect(lst), copy).then_inc(sem["s2_%d" % k], 1)
+    for k in range(2):
+        g.wait_ge(sem["c2_%d" % k], len(picks[k]))
+        sent += send(groups[k], T.slot2, T.land2, PAGE, 0, 2, True, "in_c2")
+    for k in range(2):
+        g.wait_ge(sem["s2_%d" % k], len(picks[k]))
+        sent += send(groups[k], T.slot2s, T.land2s, PAGE, 0, 2, False, "in_s2")
+    own = (PAGE * rank, PAGE * rank + PAGE)
+    lst = T.list2[:, CP * rank:CP * rank + CP]
+    v.tensor_copy(codes(T.land2[:, own[0]:own[1]]), codes(T.win[:, 0:WIDE]).indirect(lst)).then_inc(sem.own2_c, 1)
+    s.activation(T.land2s[:, own[0]:own[1]], T.wins[:, 0:WIDE].indirect(lst), copy).then_inc(sem.own2_s, 1)
+
+    g.wait_ge(sem.d_pg, 16)
+    g.partition_broadcast(T.pgb[:], T.pgrow[0:1, :], 128).then_inc(sem.pgb, 1)
+    v.wait_ge(sem.d_qw, 16)
+    v.quantize_mx(T.qwq[:], T.qws[:], T.qwt[:]).then_inc(sem.q_qw, 1)
+    wait(v, "pgb")
+    v.tensor_scalar(T.off3[:], T.pgb[:], 16.0, T.crowf[:, 0:1], AluOpType.mult, AluOpType.add).then_inc(sem.k_off3, 1)
+
+    def quarter(k):
+        return slice(64 * k, 64 * k + 64), T.off3[:, 4 * k:4 * k + 4]
+
+    wait(v, "own2_c", "k_off3")
+    v.wait_ge(sem.in_c2, arrivals[2])
+    for k in range(4):
+        cols, lst = quarter(k)
+        v.tensor_copy(codes(T.fin[:, cols]), codes(T.land2[:, 0:N * PAGE]).indirect(lst)).then_inc(sem["fc%d" % (k // 2)], 1)
+    wait(s, "own2_s", "k_off3")
+    s.wait_ge(sem.in_s2, arrivals[2])
+    wait(v, "own2_s")
+    v.wait_ge(sem.in_s2, arrivals[2])
+    for h in range(2):
+        cols, lst = quarter(2 * h)
+        s.activation(T.fins[:, cols], T.land2s[:, 0:N * PAGE].indirect(lst), copy).then_inc(sem["fs%d" % h], 1)
+        cols, lst = quarter(2 * h + 1)
+        v.tensor_copy(T.fins[:, cols], T.land2s[:, 0:N * PAGE].indirect(lst)).then_inc(sem["fs%d" % h], 1)
+    wait(t, "q_qw")
+    for h in range(2):
+        t.wait_ge(sem["fc%d" % h], 2)
+        t.wait_ge(sem["fs%d" % h], 2)
+        for o in range(O):
+            t.matmul_mx(T.acc[:, 512 * (2 * o + h):512 * (2 * o + h) + 128], T.qwq[:, 128 * o:128 * o + 128], T.qws[:, 128 * o:128 * o + 128],
+                        T.fin[:, 128 * h:128 * h + 128], T.fins[:, 128 * h:128 * h + 128], True, True).then_inc(sem["m%d%d" % (o, h)], 1)
+    for h in range(2):
+        wait(v, "m0%d" % h)
+        v.tensor_copy(T.yt[:, 128 * h:128 * h + 128], T.acc[:, 512 * h:512 * h + 128]).then_inc(sem.y0, 1)
+        wait(s, "m1%d" % h)
+        s.activation(T.yt[:, 256 + 128 * h:256 + 128 * h + 128], T.acc[:, 1024 + 512 * h:1024 + 512 * h + 128], copy).then_inc(sem.y1, 1)
+    y.wait_ge(sem.y0, 2)
+    y.dma_start(T.y[:, 0:256], T.yt[:, 0:256]).then_inc(sem.d_y, 16)
+    s.wait_ge(sem.y1, 2)
+    s.dma_start(T.y[:, 256:512], T.yt[:, 256:512]).then_inc(sem.d_y, 16)
+    y.wait_ge(sem.d_y, 32)
+    g.wait_ge(sem.sent, sent)

@@ -4,9 +4,16 @@ from concourse.mybir import dt, AluOpType, ActivationFunctionType
 N, PG, NW, SP, CW, CP, O = 8, 16, 64, 16, 16, 4, 2
 POOL = 16 * PG
 PAGE = 16 * CP
-OWN = POOL + N * CW
-WIDE = OWN + 2 * CW
+SLOTS = N * CW
+OUT = POOL + SLOTS
+WIDE = OUT + SLOTS
+TAB = POOL + 32
+DUMP = TAB + 2 * SLOTS + 32
 F8 = "float8_e4m3fn_x4"
+
+SPLIT1 = True
+QW_LATE = False
+HELP1 = False
 
 SCRATCH = {
     "nwt": ("sbuf", [128, 512], "bfloat16"),
@@ -14,37 +21,34 @@ SCRATCH = {
     "qwt": ("sbuf", [128, 512 * O], "bfloat16"),
     "nwq": ("sbuf", [128, 128], F8), "nws": ("sbuf", [128, 128], "uint8"),
     "qwq": ("sbuf", [128, 128 * O], F8), "qws": ("sbuf", [128, 128 * O], "uint8"),
-    "slot1": ("sbuf", [128, N * CW], F8), "slot1s": ("sbuf", [128, N * CW], "uint8"),
     "win": ("sbuf", [128, WIDE], F8), "wins": ("sbuf", [128, WIDE], "uint8"),
+    "hop1s": ("sbuf", [128, 2 * CW], "uint8"),
     "slot2": ("sbuf", [128, N * PAGE], F8), "slot2s": ("sbuf", [128, N * PAGE], "uint8"),
     "land2": ("sbuf", [128, N * PAGE], F8), "land2s": ("sbuf", [128, N * PAGE], "uint8"),
     "fin": ("sbuf", [128, POOL], F8), "fins": ("sbuf", [128, POOL], "uint8"),
-    "wrt": ("sbuf", [32, N * CW // 16], "int32"),
-    "wpt": ("sbuf", [32, N * CW // 16], "int32"),
+    "wrt": ("sbuf", [32, SLOTS // 16], "int32"),
+    "wpt": ("sbuf", [32, SLOTS // 16], "int32"),
     "rdt": ("sbuf", [32, N * CP // 16], "int32"),
     "pgrow": ("sbuf", [1, SP], "int32"), "pgb": ("sbuf", [128, SP], "int32"),
-    "cval": ("sbuf", [128, N * CW], "float32"),
-    "cdmp": ("sbuf", [128, N * CW // 16], "int32"),
-    "ccol": ("sbuf", [128, POOL], "float32"), "coff": ("sbuf", [128, POOL], "float32"),
-    "cmask": ("sbuf", [128, POOL], "float32"), "cnot": ("sbuf", [128, POOL], "float32"),
-    "crow": ("sbuf", [128, 1], "int32"), "crow16": ("sbuf", [128, 1], "int32"),
-    "crowp": ("sbuf", [128, 1], "float32"), "crowf": ("sbuf", [128, 1], "float32"), "crown": ("sbuf", [128, 1], "float32"),
-    "wpa": ("sbuf", [32, N * CW // 16], "int32"), "wpb": ("sbuf", [32, N * CW // 16], "int32"),
-    "comp": ("sbuf", [128, 512], "float32"),
-    "mine": ("sbuf", [128, POOL], "float32"), "last": ("sbuf", [128, POOL], "float32"),
-    "offw": ("sbuf", [128, N * CW // 16], "uint16"),
-    "offp": ("sbuf", [128, N * CW // 16], "uint16"), "offr": ("sbuf", [128, N * CP // 16], "uint16"),
+    "crow": ("sbuf", [128, 1], "int32"), "crow16": ("sbuf", [128, 1], "int32"), "crowf": ("sbuf", [128, 1], "float32"),
+    "cfirst": ("sbuf", [32, 3], "float32"), "cshift": ("sbuf", [32, 1], "float32"),
+    "cval": ("sbuf", [128, SLOTS], "bfloat16"),
+    "cdmp": ("sbuf", [128, SLOTS // 16], "int32"),
+    "wpa": ("sbuf", [32, SLOTS // 16], "int32"), "wpb": ("sbuf", [32, SLOTS // 16], "int32"),
+    "tab": ("sbuf", [128, DUMP], "bfloat16"), "turned": ("sbuf", [128, TAB], "bfloat16"),
+    "offw": ("sbuf", [128, SLOTS // 16], "uint16"),
+    "offp": ("sbuf", [128, SLOTS // 16], "uint16"), "offr": ("sbuf", [128, N * CP // 16], "uint16"),
     "list2": ("sbuf", [128, N * CP], "uint16"), "off3": ("sbuf", [128, SP], "uint16"),
     "acc": ("psum", [128, 512 * 4], "float32"),
     "yt": ("sbuf", [128, 256 * O], "float32"),
 }
 DMA_SEMS = ["d_nw", "d_wr", "d_pl", "d_wp", "d_rd", "d_pg", "d_qw", "d_y"]
-EVENTS = ["zero", "offw", "q_nw", "c1", "s1", "own_c", "own_s", "q_pl", "q_qw",
-          "i_comp", "i_col", "i_row", "k_val", "k_dmp", "k_coff", "k_mask", "k_not", "k_row", "k_rowp", "k_rowf", "k_rown",
-          "k_wpa", "k_wpb", "k_offp", "k_comp", "k_mine", "k_last", "k_offr", "k_list2", "pgb", "k_off3",
-          "c2_0", "c2_1", "s2_0", "s2_1", "own2_c", "own2_s", "fc0", "fc1", "fs0", "fs1",
-          "m00", "m01", "m10", "m11", "y0", "y1"]
-SEMAPHORES = DMA_SEMS + EVENTS + ["in_c1", "in_s1", "in_c2", "in_s2", "sent"]
+EVENTS = ["zero", "offw", "q_nw", "c1_0", "c1_1", "s1_0", "s1_1", "q_pl", "q_qw",
+          "i_row", "i_dmp", "i_val", "i_first", "k_fill", "k_shift", "k_tab", "k_idle", "k_val", "k_row", "k_rowf",
+          "k_wpa", "k_wpb", "k_offp", "k_put", "k_turn", "k_offr", "k_look", "k_list2", "pgb", "k_off3",
+          "c2_0", "c2_1", "c2_2", "s2_0", "s2_1", "own2_c", "own2_s", "fc0", "fc1", "fs0", "fs1",
+          "m00", "m01", "m10", "m11", "y00", "y01", "y10", "y11"]
+SEMAPHORES = DMA_SEMS + EVENTS + ["in_c1", "in_s1", "in_c2", "in_s2", "fed1", "sent"]
 
 
 def kinds(src, cores, topo):
@@ -54,18 +58,51 @@ def kinds(src, cores, topo):
     return near, [d for d in off if d not in near], peer
 
 
+def helpers(src, cores, topo):
+    far = kinds(src, cores, topo)[1]
+    free = [c for c in topo.cores_of(src) if c not in cores and topo.die(c) == topo.die(src)]
+    first = [c for c in free if topo.may_write(c, far[0])][0]
+    return first, [c for c in free if c != first][0]
+
+
+def deal(dests, engines):
+    n = len(engines) // len(dests)
+    return [(d, engines[n * i:n * i + n]) for i, d in enumerate(dests)]
+
+
 def plan(src, cores, topo):
     near, far, peer = kinds(src, cores, topo)
+    mate, plane = near[:len(near) // 2], near[len(near) // 2:]
     e = topo.engines(src, near[0])
-    a, b = e[0::2], e[1::2]
-    out = {}
-    for i, d in enumerate(near):
-        out[d] = ([a[i]], [b[i]], e[2 * i:2 * i + 2])
-    for i, d in enumerate(far):
-        out[d] = (b[2 * i:2 * i + 2], a[2 * i:2 * i + 2], e[4 * i:4 * i + 4])
-    for d in peer:
-        rest = [x for x in topo.engines(src, d) if x not in e]
-        out[d] = ([rest[0]], [rest[2]], [rest[0], rest[2]])
+    rest = [x for x in topo.engines(src, peer[0]) if x not in e]
+    me = cores.index(src)
+    to_peer = [(peer[0], [rest[0], rest[2]])]
+    to_near = deal(mate, e[0::2]) + deal(plane, e[1::2])
+
+    def new(pairs, buf, s):
+        return [(d, es, buf, OUT + CW * cores.index(d), buf, POOL + CW * me, CW, s) for d, es in pairs]
+
+    def pages(pairs, a, b, s):
+        return [(d, es, a, PAGE * cores.index(d), b, PAGE * me, PAGE, s) for d, es in pairs]
+
+    out = {src: [("c1_far", new(deal(far, e), "win", "in_c1")),
+                 ("c1_near", new(to_near + to_peer, "win", "in_c1"))]}
+    if HELP1:
+        ha, hb = helpers(src, cores, topo)
+        ways = ((ha, far, rest[4:8]), (hb, plane, [rest[1], rest[3]]))
+        out[src] += [("s1_help", [(h, es, "wins", OUT + CW * cores.index(ds[0]), "hop1s", 0, 2 * CW, "fed1") for h, ds, es in ways]),
+                     ("s1_rest", new(deal(mate, e) + to_peer, "wins", "in_s1"))]
+        for h, ds, es in ways:
+            out[h] = [("fed1", [(d, es, "hop1s", CW * i, "wins", POOL + CW * me, CW, "in_s1")
+                                for i, (d, es) in enumerate(deal(ds, topo.engines(h, ds[0])))])]
+    else:
+        out[src] += [("s1_far", new(deal(far, e), "wins", "in_s1")),
+                     ("s1_near", new(to_near + to_peer, "wins", "in_s1"))]
+    out[src] += [("c2_far", pages(deal(far, e), "slot2", "land2", "in_c2")),
+                 ("c2_near", pages(to_near, "slot2", "land2", "in_c2")),
+                 ("c2_peer", pages(to_peer, "slot2", "land2", "in_c2")),
+                 ("s2_far", pages(deal(far, e), "slot2s", "land2s", "in_s2")),
+                 ("s2_near", pages(to_near + to_peer, "slot2s", "land2s", "in_s2"))]
     return out
 
 
@@ -80,18 +117,43 @@ def runs(ranks):
 
 
 def rank_program(g, core, T, topo):
+    sem = T.sem
+    cores = list(T.cores)
+    calls, arrivals = {}, {}
+    for c in cores:
+        calls.update(plan(c, cores, topo))
+    if core not in calls:
+        return
+    for cs in calls.values():
+        for name, writes in cs:
+            for w in writes:
+                if w[0] == core:
+                    arrivals[w[7]] = arrivals.get(w[7], 0) + len(w[1])
+    mine_calls = dict(calls[core])
+
+    def send(name):
+        tr = []
+        for d, es, src, at, dst, to, n, arrive in mine_calls[name]:
+            rid, pid = topo.addr(d, core)
+            a, b = T[src][:, at:at + n], T[dst][:, to:to + n]
+            if SCRATCH[src][2] == F8:
+                a, b = a.bitcast(dt.uint8), b.bitcast(dt.uint8)
+            tr.append(RemoteDMATransfer(dst_ids=[DstId(rid=rid, pnc=pid)], dma_engine_mask=sum(1 << e for e in es),
+                                        remote_sem=sem[arrive], src=a, dst=b))
+        g.remote_dma_fused(tr, local_sem=sem.sent)
+
+    sent = sum(len(w[1]) for ws in mine_calls.values() for w in ws)
     rank = T.rank_of(core)
     if rank is None:
+        for name in mine_calls:
+            g.wait_ge(sem[name], arrivals[name])
+            send(name)
+        g.wait_ge(sem.sent, sent)
         return
-    sem = T.sem
     v, s, y, t = g.vector, g.scalar, g.sync, g.tensor
-    fn = ActivationFunctionType
-    copy = fn.Copy
-    cores = list(T.cores)
+    op = AluOpType
+    copy = ActivationFunctionType.Copy
     near, far, peer = kinds(core, cores, topo)
-    ways = plan(core, cores, topo)
-    came = [plan(d, cores, topo)[core] for d in cores if d != core]
-    arrivals = [sum(len(w[k]) for w in came) for k in range(3)]
 
     def wait(q, *names):
         for n in names:
@@ -103,138 +165,140 @@ def rank_program(g, core, T, topo):
     y.dma_start(T.nwt[:, 0:4 * NW], T.nw[:]).then_inc(sem.d_nw, 16)
     for k in range(2):
         s.dma_start(T.wrt[16 * k:16 * k + 16, :], T.wr[:]).then_inc(sem.d_wr, 16)
-    s.dma_start(T.plt[:], T.pl[:]).then_inc(sem.d_pl, 16)
     for k in range(2):
         y.dma_start(T.wpt[16 * k:16 * k + 16, :], T.wp[:]).then_inc(sem.d_wp, 16)
-    for k in range(2):
-        y.dma_start(T.rdt[16 * k:16 * k + 16, :], T.rd[:]).then_inc(sem.d_rd, 16)
+        s.dma_start(T.rdt[16 * k:16 * k + 16, :], T.rd[:]).then_inc(sem.d_rd, 16)
+    y.dma_start(T.plt[:], T.pl[:]).then_inc(sem.d_pl, 16)
     y.dma_start(T.pgrow[0:1, :], T.pg[:]).then_inc(sem.d_pg, 16)
-    y.dma_start(T.qwt[:], T.qw[:]).then_inc(sem.d_qw, 16)
+    if not QW_LATE:
+        y.dma_start(T.qwt[:], T.qw[:]).then_inc(sem.d_qw, 16)
 
     fl = dict(allow_small_or_imprecise_dtypes=True)
+    g.iota(T.cval[:], [[1, SLOTS]], 0, 0, **fl).then_inc(sem.i_val, 1)
+    g.iota(T.cfirst[:], [[SLOTS, 3]], -POOL - 16, 1, **fl).then_inc(sem.i_first, 1)
+    g.iota(T.cdmp[:], [[16, SLOTS // 16]], TAB, 1).then_inc(sem.i_dmp, 1)
     g.iota(T.crow[:], [[0, 1]], 0, 1).then_inc(sem.i_row, 1)
-    g.iota(T.comp[:, 0:POOL], [[1, POOL]], 0, 0, **fl).then_inc(sem.i_comp, 1)
-    g.iota(T.ccol[:], [[0, 16], [1, 16]], 0, 0, **fl).then_inc(sem.i_col, 1)
     v.memset(T.nwt[:, 4 * NW:512], 0.0).then_inc(sem.zero, 1)
-    wait(v, "i_row")
-    v.tensor_scalar(T.crow16[:], T.crow[:], 15, None, AluOpType.bitwise_and).then_inc(sem.k_row, 1)
-    v.tensor_copy(T.crowp[:], T.crow[:]).then_inc(sem.k_rowp, 1)
-    wait(v, "k_row")
-    v.tensor_copy(T.crowf[:], T.crow16[:]).then_inc(sem.k_rowf, 1)
-    wait(v, "k_rowf")
-    v.tensor_scalar(T.crown[:], T.crowf[:], -1.0, None, AluOpType.mult).then_inc(sem.k_rown, 1)
-    wait(v, "i_comp", "k_rowp")
-    odd = CW * (rank % 2)
-    pieces = [p for p in ((0, CW * rank, POOL), (CW * rank, CW * rank + CW, OWN + odd - CW * rank), (CW * rank + CW, N * CW, POOL)) if p[0] < p[1]]
-    for a, b, add in pieces:
-        v.tensor_scalar(T.cval[:, a:b], T.comp[:, a:b], float(add), None, AluOpType.add).then_inc(sem.k_val, 1)
-    v.tensor_scalar(T.cdmp[:], T.comp[:, 0:N * CW:16], T.crowp[:, 0:1], float(POOL), AluOpType.add, AluOpType.add).then_inc(sem.k_dmp, 1)
+    v.memset(T.turned[:, 0:32], 0.0).then_inc(sem.k_fill, 1)
+    v.memset(T.offr[:], 0).then_inc(sem.k_fill, 1)
+    wait(s, "i_val", "i_first")
+    for k in range(3):
+        n = min(SLOTS, TAB - SLOTS * k)
+        s.activation(T.tab[0:32, SLOTS * k:SLOTS * k + n], T.cval[0:32, 0:n], ActivationFunctionType.Identity,
+                     bias=T.cfirst[:, k:k + 1]).then_inc(sem.k_tab, 1)
 
+    groups1 = [far, near + peer] if SPLIT1 else [far + near + peer]
+    picks1 = [runs([T.rank_of(d) for d in ds] + ([rank] if peer[0] in ds else [])) for ds in groups1]
     v.wait_ge(sem.d_wr, 32)
     for k in range(4):
         v.tensor_copy(T.offw[32 * k:32 * k + 32, :], T.wrt[:]).then_inc(sem.offw, 1)
     v.wait_ge(sem.d_nw, 16)
     wait(v, "zero")
     v.quantize_mx(T.nwq[:], T.nws[:], T.nwt[:]).then_inc(sem.q_nw, 1)
-    v.wait_ge(sem.offw, 4)
-    wait(v, "q_nw")
-    v.tensor_copy(codes(T.slot1[:, 0:N * CW]), codes(T.nwq[:, 0:NW]).indirect(T.offw[:, 0:8])).then_inc(sem.c1, 1)
-    s.wait_ge(sem.offw, 4)
-    wait(s, "q_nw")
-    s.activation(T.slot1s[:, 0:N * CW], T.nws[:, 0:NW].indirect(T.offw[:, 0:8]), copy).then_inc(sem.s1, 1)
+    for q in (v, s):
+        q.wait_ge(sem.offw, 4)
+        wait(q, "q_nw")
+    for k, ps in enumerate(picks1):
+        for a, b in ps:
+            cols, lst = slice(OUT + CW * a, OUT + CW * b), T.offw[:, a:b]
+            v.tensor_copy(codes(T.win[:, cols]), codes(T.nwq[:, 0:NW]).indirect(lst)).then_inc(sem["c1_%d" % k], 1)
+            s.activation(T.wins[:, cols], T.nws[:, 0:NW].indirect(lst), copy).then_inc(sem["s1_%d" % k], 1)
 
-    def send(dests, src, dst, width, base, part, bits, arrive):
-        tr = []
-        for d in dests:
-            q = T.rank_of(d)
-            rid, pid = topo.addr(d, core)
-            a, b = src[:, width * q:width * q + width], dst[:, base + width * rank:base + width * rank + width]
-            if bits:
-                a, b = a.bitcast(dt.uint8), b.bitcast(dt.uint8)
-            tr.append(RemoteDMATransfer(dst_ids=[DstId(rid=rid, pnc=pid)], dma_engine_mask=sum(1 << e for e in ways[d][part]),
-                                        remote_sem=sem[arrive], src=a, dst=b))
-        g.remote_dma_fused(tr, local_sem=sem.sent)
-        return sum(len(ways[d][part]) for d in dests)
+    for k, name in enumerate(("c1_far", "c1_near")):
+        g.wait_ge(sem["c1_%d" % k], len(picks1[k]))
+        send(name)
+    if HELP1:
+        for k in range(2):
+            g.wait_ge(sem["s1_%d" % k], len(picks1[k]))
+        send("s1_help")
+        send("s1_rest")
+    else:
+        for k, name in enumerate(("s1_far", "s1_near")):
+            g.wait_ge(sem["s1_%d" % k], len(picks1[k]))
+            send(name)
 
-    sent = 0
-    wait(g, "c1")
-    sent += send(far + near + peer, T.slot1, T.win, CW, POOL, 0, True, "in_c1")
-    wait(g, "s1")
-    sent += send(far + near + peer, T.slot1s, T.wins, CW, POOL, 1, False, "in_s1")
-
-    lst = T.offw[:, rank - rank % 2:rank - rank % 2 + 2]
-    v.tensor_copy(codes(T.win[:, OWN:WIDE]), codes(T.nwq[:, 0:NW]).indirect(lst)).then_inc(sem.own_c, 1)
-    s.activation(T.wins[:, OWN:WIDE], T.nws[:, 0:NW].indirect(lst), copy).then_inc(sem.own_s, 1)
-
-    wait(s, "i_col", "k_rown")
-    s.activation(T.coff[:], T.ccol[:], fn.Square, bias=T.crown[:, 0:1]).then_inc(sem.k_coff, 1)
-    wait(s, "k_coff")
-    s.activation(T.cmask[:], T.coff[:], fn.Relu, bias=1.0, scale=-1.0).then_inc(sem.k_mask, 1)
-    s.activation(T.cnot[:], T.coff[:], fn.Sign).then_inc(sem.k_not, 1)
+    mine = T.cval[:, CW * rank:CW * rank + CW]
     v.wait_ge(sem.d_wp, 32)
-    v.tensor_scalar(T.wpa[:], T.wpt[:], 4095, None, AluOpType.bitwise_and).then_inc(sem.k_wpa, 1)
-    wait(v, "k_wpa", "k_dmp")
-    v.tensor_tensor(T.wpb[:], T.wpa[:], T.cdmp[0:32, :], AluOpType.min).then_inc(sem.k_wpb, 1)
-    wait(v, "k_wpb")
-    for k in range(4):
-        v.tensor_copy(T.offp[32 * k:32 * k + 32, :], T.wpb[:]).then_inc(sem.k_offp, 1)
-    v.wait_ge(sem.k_val, len(pieces))
-    v.wait_ge(sem.k_offp, 4)
-    v.tensor_copy(T.comp[:, 0:512].indirect(T.offp[:, 0:8]), T.cval[:]).then_inc(sem.k_comp, 1)
+    v.tensor_scalar(T.wpa[:], T.wpt[:], 4095, None, op.bitwise_and).then_inc(sem.k_wpa, 1)
+    wait(v, "i_first")
+    v.tensor_scalar(T.cshift[:], T.cfirst[:, 0:1], float(-POOL), 16.0, op.is_lt, op.mult).then_inc(sem.k_shift, 1)
+    wait(v, "i_dmp")
+    v.tensor_copy(T.offp[:], T.cdmp[:]).then_inc(sem.k_idle, 1)
+    wait(v, "k_wpa")
+    v.tensor_tensor(T.wpb[:], T.wpa[:], T.cdmp[0:32, :], op.min).then_inc(sem.k_wpb, 1)
+    v.wait_ge(sem.k_tab, 3)
+    v.tensor_scalar(mine, mine, float(SLOTS), None, op.add).then_inc(sem.k_val, 1)
+    wait(v, "k_wpb", "k_idle", "k_shift")
+    v.tensor_scalar(T.offp[0:32, :], T.wpb[:], T.cshift[:, 0:1], None, op.add).then_inc(sem.k_offp, 1)
     v.wait_ge(sem.d_rd, 32)
-    for k in range(4):
-        v.tensor_scalar(T.offr[32 * k:32 * k + 32, :], T.rdt[:], 16, 15, AluOpType.mult, AluOpType.add).then_inc(sem.k_offr, 1)
-    wait(v, "k_mask", "k_comp")
-    v.tensor_tensor(T.mine[:], T.comp[:, 0:POOL], T.cmask[:], AluOpType.mult).then_inc(sem.k_mine, 1)
-    wait(v, "k_mine", "k_not")
-    v.tensor_tensor_scan(T.last[:], T.cnot[:], T.mine[:], 0.0, AluOpType.mult, AluOpType.add).then_inc(sem.k_last, 1)
-    wait(v, "k_last")
-    v.wait_ge(sem.k_offr, 4)
-    v.tensor_copy(T.list2[:], T.last[:, 0:POOL].indirect(T.offr[:, 0:2])).then_inc(sem.k_list2, 1)
+    v.wait_ge(sem.k_fill, 2)
+    v.tensor_scalar(T.offr[0:32, :], T.rdt[:], 16.0, T.cshift[:, 0:1], op.mult, op.add).then_inc(sem.k_offr, 1)
+    wait(v, "k_offp", "k_val")
+    v.tensor_copy(T.tab[:, 0:DUMP].indirect(T.offp[:, 0:8]), T.cval[:]).then_inc(sem.k_put, 1)
+    wait(v, "k_put")
+    v.transpose(T.turned[0:32, :], T.tab[0:32, 0:TAB]).then_inc(sem.k_turn, 1)
     v.wait_ge(sem.d_pl, 16)
-    v.quantize_mx(T.win[:, 0:POOL], T.wins[:, 0:POOL], T.plt[:]).then_inc(sem.q_pl, 1)
+    v.quantize_mx(T.win[:, 0:128], T.wins[:, 0:128], T.plt[:, 0:512]).then_inc(sem.q_pl, 1)
+    wait(v, "k_turn", "k_offr")
+    v.tensor_scalar(T.list2[:], T.turned[:, 0:TAB].indirect(T.offr[:, 0:2]), float(POOL), None, op.add).then_inc(sem.k_look, 1)
+    v.quantize_mx(T.win[:, 128:POOL], T.wins[:, 128:POOL], T.plt[:, 512:4 * POOL]).then_inc(sem.q_pl, 1)
+    wait(v, "k_look")
+    for k in range(1, 4):
+        v.tensor_copy(T.list2[32 * k:32 * k + 32, :], T.list2[0:32, :]).then_inc(sem.k_list2, 1)
 
-    groups = [far, near + peer]
-    picks = [runs([T.rank_of(d) for d in ds]) for ds in groups]
-    wait(v, "k_list2", "q_pl", "own_c")
-    v.wait_ge(sem.in_c1, arrivals[0])
-    wait(s, "k_list2", "q_pl", "own_s")
-    s.wait_ge(sem.in_s1, arrivals[1])
-    for k in range(2):
-        for a, b in picks[k]:
-            lst = T.list2[:, CP * a:CP * b]
-            v.tensor_copy(codes(T.slot2[:, PAGE * a:PAGE * b]), codes(T.win[:, 0:WIDE]).indirect(lst)).then_inc(sem["c2_%d" % k], 1)
-            s.activation(T.slot2s[:, PAGE * a:PAGE * b], T.wins[:, 0:WIDE].indirect(lst), copy).then_inc(sem["s2_%d" % k], 1)
-    for k in range(2):
-        g.wait_ge(sem["c2_%d" % k], len(picks[k]))
-        sent += send(groups[k], T.slot2, T.land2, PAGE, 0, 2, True, "in_c2")
-    for k in range(2):
-        g.wait_ge(sem["s2_%d" % k], len(picks[k]))
-        sent += send(groups[k], T.slot2s, T.land2s, PAGE, 0, 2, False, "in_s2")
-    own = (PAGE * rank, PAGE * rank + PAGE)
-    lst = T.list2[:, CP * rank:CP * rank + CP]
-    v.tensor_copy(codes(T.land2[:, own[0]:own[1]]), codes(T.win[:, 0:WIDE]).indirect(lst)).then_inc(sem.own2_c, 1)
-    s.activation(T.land2s[:, own[0]:own[1]], T.wins[:, 0:WIDE].indirect(lst), copy).then_inc(sem.own2_s, 1)
+    def ready(q, kind, n):
+        q.wait_ge(sem.k_list2, 3)
+        q.wait_ge(sem.q_pl, 2)
+        for k, ps in enumerate(picks1):
+            q.wait_ge(sem["%s1_%d" % (kind, k)], len(ps))
+        q.wait_ge(sem["in_%s1" % kind], arrivals["in_%s1" % kind])
 
+    def pick(q, ds, bits, done):
+        (a, b), = runs([T.rank_of(d) for d in ds])
+        cols, lst = slice(PAGE * a, PAGE * b), T.list2[:, CP * a:CP * b]
+        if bits:
+            call = q.tensor_copy(codes((T.land2 if core in ds else T.slot2)[:, cols]), codes(T.win[:, 0:WIDE]).indirect(lst))
+        elif q is v:
+            call = q.tensor_copy((T.land2s if core in ds else T.slot2s)[:, cols], T.wins[:, 0:WIDE].indirect(lst))
+        else:
+            call = q.activation((T.land2s if core in ds else T.slot2s)[:, cols], T.wins[:, 0:WIDE].indirect(lst), copy)
+        call.then_inc(sem[done], 1)
+
+    half = len(near) // 2
+    ready(v, "c", 0)
+    for ds, done in ((far, "c2_0"), (near[:half], "c2_1"), (near[half:], "c2_1"), (peer, "c2_2"), ([core], "own2_c")):
+        pick(v, ds, True, done)
+    ready(s, "s", 1)
+    for ds, done in ((far, "s2_0"), (near[:half], "s2_1"), (peer, "s2_1"), ([core], "own2_s")):
+        pick(s, ds, False, done)
+    ready(v, "s", 1)
+    pick(v, near[half:], False, "s2_1")
+    for name, done, n in (("c2_far", "c2_0", 1), ("c2_near", "c2_1", 2), ("c2_peer", "c2_2", 1), ("s2_far", "s2_0", 1), ("s2_near", "s2_1", 3)):
+        g.wait_ge(sem[done], n)
+        send(name)
     g.wait_ge(sem.d_pg, 16)
     g.partition_broadcast(T.pgb[:], T.pgrow[0:1, :], 128).then_inc(sem.pgb, 1)
+    wait(v, "i_row")
+    v.tensor_scalar(T.crow16[:], T.crow[:], 15, None, op.bitwise_and).then_inc(sem.k_row, 1)
     v.wait_ge(sem.d_qw, 16)
     v.quantize_mx(T.qwq[:], T.qws[:], T.qwt[:]).then_inc(sem.q_qw, 1)
-    wait(v, "pgb")
-    v.tensor_scalar(T.off3[:], T.pgb[:], 16.0, T.crowf[:, 0:1], AluOpType.mult, AluOpType.add).then_inc(sem.k_off3, 1)
+    wait(v, "k_row")
+    v.tensor_copy(T.crowf[:], T.crow16[:]).then_inc(sem.k_rowf, 1)
+    wait(v, "pgb", "k_rowf")
+    v.tensor_scalar(T.off3[:], T.pgb[:], 16.0, T.crowf[:, 0:1], op.mult, op.add).then_inc(sem.k_off3, 1)
 
     def quarter(k):
         return slice(64 * k, 64 * k + 64), T.off3[:, 4 * k:4 * k + 4]
 
     wait(v, "own2_c", "k_off3")
-    v.wait_ge(sem.in_c2, arrivals[2])
+    v.wait_ge(sem.in_c2, arrivals["in_c2"])
     for k in range(4):
         cols, lst = quarter(k)
         v.tensor_copy(codes(T.fin[:, cols]), codes(T.land2[:, 0:N * PAGE]).indirect(lst)).then_inc(sem["fc%d" % (k // 2)], 1)
     wait(s, "own2_s", "k_off3")
-    s.wait_ge(sem.in_s2, arrivals[2])
+    s.wait_ge(sem.in_s2, arrivals["in_s2"])
     wait(v, "own2_s")
-    v.wait_ge(sem.in_s2, arrivals[2])
+    v.wait_ge(sem.in_s2, arrivals["in_s2"])
     for h in range(2):
         cols, lst = quarter(2 * h)
         s.activation(T.fins[:, cols], T.land2s[:, 0:N * PAGE].indirect(lst), copy).then_inc(sem["fs%d" % h], 1)
@@ -248,13 +312,13 @@ def rank_program(g, core, T, topo):
             t.matmul_mx(T.acc[:, 512 * (2 * o + h):512 * (2 * o + h) + 128], T.qwq[:, 128 * o:128 * o + 128], T.qws[:, 128 * o:128 * o + 128],
                         T.fin[:, 128 * h:128 * h + 128], T.fins[:, 128 * h:128 * h + 128], True, True).then_inc(sem["m%d%d" % (o, h)], 1)
     for h in range(2):
-        wait(v, "m0%d" % h)
-        v.tensor_copy(T.yt[:, 128 * h:128 * h + 128], T.acc[:, 512 * h:512 * h + 128]).then_inc(sem.y0, 1)
-        wait(s, "m1%d" % h)
-        s.activation(T.yt[:, 256 + 128 * h:256 + 128 * h + 128], T.acc[:, 1024 + 512 * h:1024 + 512 * h + 128], copy).then_inc(sem.y1, 1)
-    y.wait_ge(sem.y0, 2)
-    y.dma_start(T.y[:, 0:256], T.yt[:, 0:256]).then_inc(sem.d_y, 16)
-    s.wait_ge(sem.y1, 2)
-    s.dma_start(T.y[:, 256:512], T.yt[:, 256:512]).then_inc(sem.d_y, 16)
-    y.wait_ge(sem.d_y, 32)
+        wait(s, "m0%d" % h)
+        s.activation(T.yt[:, 128 * h:128 * h + 128], T.acc[:, 512 * h:512 * h + 128], copy).then_inc(sem["y0%d" % h], 1)
+        wait(v, "m1%d" % h)
+        v.tensor_copy(T.yt[:, 256 + 128 * h:256 + 128 * h + 128], T.acc[:, 1024 + 512 * h:1024 + 512 * h + 128]).then_inc(sem["y1%d" % h], 1)
+    for q, o, h in ((y, 0, 0), (y, 1, 0), (s, 0, 1), (y, 1, 1)):
+        cols = slice(256 * o + 128 * h, 256 * o + 128 * h + 128)
+        wait(q, "y%d%d" % (o, h))
+        q.dma_start(T.y[:, cols], T.yt[:, cols]).then_inc(sem.d_y, 16)
+    y.wait_ge(sem.d_y, 64)
     g.wait_ge(sem.sent, sent)

@@ -13,7 +13,7 @@ F8 = "float8_e4m3fn_x4"
 
 SPLIT1 = True
 QW_LATE = False
-HELP1 = False
+RELAY = False
 
 SCRATCH = {
     "nwt": ("sbuf", [128, 512], "bfloat16"),
@@ -23,10 +23,11 @@ SCRATCH = {
     "qwq": ("sbuf", [128, 128 * O], F8), "qws": ("sbuf", [128, 128 * O], "uint8"),
     "win": ("sbuf", [128, WIDE], F8), "wins": ("sbuf", [128, WIDE], "uint8"),
     "hop1s": ("sbuf", [128, 2 * CW], "uint8"),
+    "hop2": ("sbuf", [128, 2 * PAGE], F8), "hop2s": ("sbuf", [128, 2 * PAGE], "uint8"),
     "slot2": ("sbuf", [128, N * PAGE], F8), "slot2s": ("sbuf", [128, N * PAGE], "uint8"),
     "land2": ("sbuf", [128, N * PAGE], F8), "land2s": ("sbuf", [128, N * PAGE], "uint8"),
     "fin": ("sbuf", [128, POOL], F8), "fins": ("sbuf", [128, POOL], "uint8"),
-    "wrt": ("sbuf", [32, SLOTS // 16], "int32"),
+    "wrt": ("sbuf", [64, SLOTS // 16], "int32"),
     "wpt": ("sbuf", [32, SLOTS // 16], "int32"),
     "rdt": ("sbuf", [32, N * CP // 16], "int32"),
     "pgrow": ("sbuf", [1, SP], "int32"), "pgb": ("sbuf", [128, SP], "int32"),
@@ -46,9 +47,9 @@ DMA_SEMS = ["d_nw", "d_wr", "d_pl", "d_wp", "d_rd", "d_pg", "d_qw", "d_y"]
 EVENTS = ["zero", "offw", "q_nw", "c1_0", "c1_1", "s1_0", "s1_1", "q_pl", "q_qw",
           "i_row", "i_dmp", "i_val", "i_first", "k_fill", "k_shift", "k_tab", "k_idle", "k_val", "k_row", "k_rowf",
           "k_wpa", "k_wpb", "k_offp", "k_put", "k_turn", "k_offr", "k_look", "k_list2", "pgb", "k_off3",
-          "c2_0", "c2_1", "c2_2", "s2_0", "s2_1", "own2_c", "own2_s", "fc0", "fc1", "fs0", "fs1",
+          "c2_0", "c2_1", "c2_2", "c2_3", "c2_4", "s2_0", "s2_1", "s2_2", "s2_3", "own2_c", "own2_s", "fc0", "fc1", "fs0", "fs1",
           "m00", "m01", "m10", "m11", "y00", "y01", "y10", "y11"]
-SEMAPHORES = DMA_SEMS + EVENTS + ["in_c1", "in_s1", "in_c2", "in_s2", "fed1", "sent"]
+SEMAPHORES = DMA_SEMS + EVENTS + ["in_c1", "in_s1", "in_c2", "in_s2", "fed1", "fed2", "fed3", "sent"]
 
 
 def kinds(src, cores, topo):
@@ -76,8 +77,9 @@ def plan(src, cores, topo):
     e = topo.engines(src, near[0])
     rest = [x for x in topo.engines(src, peer[0]) if x not in e]
     me = cores.index(src)
-    to_peer = [(peer[0], [rest[0], rest[2]])]
-    to_near = deal(mate, e[0::2]) + deal(plane, e[1::2])
+    to_peer = [(peer[0], rest[0::2])]
+    to_near = deal(mate, e[0::2]) + deal(plane[::-1], e[1::2])
+    to_far = deal(far, e[0::2] + e[1::2])
 
     def new(pairs, buf, s):
         return [(d, es, buf, OUT + CW * cores.index(d), buf, POOL + CW * me, CW, s) for d, es in pairs]
@@ -85,24 +87,33 @@ def plan(src, cores, topo):
     def pages(pairs, a, b, s):
         return [(d, es, a, PAGE * cores.index(d), b, PAGE * me, PAGE, s) for d, es in pairs]
 
-    out = {src: [("c1_far", new(deal(far, e), "win", "in_c1")),
-                 ("c1_near", new(to_near + to_peer, "win", "in_c1"))]}
-    if HELP1:
-        ha, hb = helpers(src, cores, topo)
-        ways = ((ha, far, rest[4:8]), (hb, plane, [rest[1], rest[3]]))
-        out[src] += [("s1_help", [(h, es, "wins", OUT + CW * cores.index(ds[0]), "hop1s", 0, 2 * CW, "fed1") for h, ds, es in ways]),
-                     ("s1_rest", new(deal(mate, e) + to_peer, "wins", "in_s1"))]
-        for h, ds, es in ways:
-            out[h] = [("fed1", [(d, es, "hop1s", CW * i, "wins", POOL + CW * me, CW, "in_s1")
-                                for i, (d, es) in enumerate(deal(ds, topo.engines(h, ds[0])))])]
-    else:
-        out[src] += [("s1_far", new(deal(far, e), "wins", "in_s1")),
-                     ("s1_near", new(to_near + to_peer, "wins", "in_s1"))]
-    out[src] += [("c2_far", pages(deal(far, e), "slot2", "land2", "in_c2")),
-                 ("c2_near", pages(to_near, "slot2", "land2", "in_c2")),
-                 ("c2_peer", pages(to_peer, "slot2", "land2", "in_c2")),
-                 ("s2_far", pages(deal(far, e), "slot2s", "land2s", "in_s2")),
-                 ("s2_near", pages(to_near + to_peer, "slot2s", "land2s", "in_s2"))]
+    far, mate, plane = [sorted(ds, key=lambda d: topo.die(d) != topo.die(src)) for ds in (far, mate, plane)]
+
+    def steps(a, b, at=2, inside=rest):
+        out = [[(far[1], a), (far[0], b)], [(mate[1], a), (plane[1], b)], [(plane[0], a), (mate[0], b)]]
+        out[at] += [(peer[0], inside)]
+        return out
+
+    out = {src: [("c1_%d" % k, new(ws, "win", "in_c1")) for k, ws in enumerate(steps(e[0::2], e[1::2], 2, rest[0::2]))]}
+    a, b = e[0::2], e[1::2]
+    rest = rest[0::2]
+    out = {src: [("c1_%d" % k, new(ws, "win", "in_c1")) for k, ws in enumerate(
+        [[(far[1], a)], [(far[0], b)], [(plane[1], a), (plane[0], b), (peer[0], rest)], [(mate[1], a), (mate[0], b)]])]}
+    out[src] += [("s1_0", new(to_far, "wins", "in_s1")), ("s1_1", new(to_near + [(peer[0], rest)], "wins", "in_s1"))]
+    out[src] += [("c2_%d" % k, pages(ws, "slot2", "land2", "in_c2")) for k, ws in enumerate(
+        [[(far[1], a)], [(far[0], b)], [(plane[1], a), (mate[1], b)], [(plane[0], a), (mate[0], b), (peer[0], rest)]])]
+    out[src] += [("s2_%d" % k, pages(ws, "slot2s", "land2s", "in_s2")) for k, ws in enumerate(
+        [[(far[1], b), (far[0], a)], [(plane[1], a), (plane[0], b), (peer[0], rest)], [(mate[1], e)], [(mate[0], e)]])]
+    if RELAY:
+        h = [c for c in topo.cores_of(mate[0]) if c not in cores and topo.die(c) == topo.die(src)][0]
+        out[h] = []
+        calls = dict(out[src])
+        for name, hop, fed in (("s1_0", "hop1s", "fed1"), ("c2_0", "hop2", "fed2")):
+            ws = sorted(calls[name], key=lambda w: w[3])
+            calls[name] = [(h, e, ws[0][2], ws[0][3], hop, 0, 2 * ws[0][6], fed)]
+            eh = topo.engines(h, far[0])
+            out[h].append((fed, [(w[0], eh[i::2], hop, w[6] * i, w[4], w[5], w[6], w[7]) for i, w in enumerate(ws)]))
+        out[src] = list(calls.items())
     return out
 
 
@@ -127,19 +138,19 @@ def rank_program(g, core, T, topo):
     for cs in calls.values():
         for name, writes in cs:
             for w in writes:
-                if w[0] == core:
+                if core in (w[0] if isinstance(w[0], tuple) else (w[0],)):
                     arrivals[w[7]] = arrivals.get(w[7], 0) + len(w[1])
     mine_calls = dict(calls[core])
 
     def send(name):
         tr = []
         for d, es, src, at, dst, to, n, arrive in mine_calls[name]:
-            rid, pid = topo.addr(d, core)
+            ids = [topo.addr(x, core) for x in (d if isinstance(d, tuple) else (d,))]
             a, b = T[src][:, at:at + n], T[dst][:, to:to + n]
             if SCRATCH[src][2] == F8:
                 a, b = a.bitcast(dt.uint8), b.bitcast(dt.uint8)
-            tr.append(RemoteDMATransfer(dst_ids=[DstId(rid=rid, pnc=pid)], dma_engine_mask=sum(1 << e for e in es),
-                                        remote_sem=sem[arrive], src=a, dst=b))
+            tr.append(RemoteDMATransfer(dst_ids=[DstId(rid=rid, pnc=pid) for rid, pid in ids], dma_engine_mask=sum(1 << e for e in es),
+                                        remote_sem=sem[arrive], srcs=[a], dsts=[b for x in ids]))
         g.remote_dma_fused(tr, local_sem=sem.sent)
 
     sent = sum(len(w[1]) for ws in mine_calls.values() for w in ws)
@@ -163,40 +174,42 @@ def rank_program(g, core, T, topo):
         return view.bitcast(dt.uint32)
 
     y.dma_start(T.nwt[:, 0:4 * NW], T.nw[:]).then_inc(sem.d_nw, 16)
+    for k in range(4):
+        (s if k < 2 else y).dma_start(T.wrt[16 * k:16 * k + 16, :], T.wr[:]).then_inc(sem.d_wr, 16)
     for k in range(2):
-        s.dma_start(T.wrt[16 * k:16 * k + 16, :], T.wr[:]).then_inc(sem.d_wr, 16)
-    for k in range(2):
-        y.dma_start(T.wpt[16 * k:16 * k + 16, :], T.wp[:]).then_inc(sem.d_wp, 16)
-        s.dma_start(T.rdt[16 * k:16 * k + 16, :], T.rd[:]).then_inc(sem.d_rd, 16)
-    y.dma_start(T.plt[:], T.pl[:]).then_inc(sem.d_pl, 16)
+        s.dma_start(T.wpt[16 * k:16 * k + 16, :], T.wp[:]).then_inc(sem.d_wp, 16)
+        y.dma_start(T.rdt[16 * k:16 * k + 16, :], T.rd[:]).then_inc(sem.d_rd, 16)
+    s.dma_start(T.plt[:], T.pl[:]).then_inc(sem.d_pl, 16)
+    y.dma_start(T.qwt[:], T.qw[:]).then_inc(sem.d_qw, 16)
     y.dma_start(T.pgrow[0:1, :], T.pg[:]).then_inc(sem.d_pg, 16)
-    if not QW_LATE:
-        y.dma_start(T.qwt[:], T.qw[:]).then_inc(sem.d_qw, 16)
 
     fl = dict(allow_small_or_imprecise_dtypes=True)
-    g.iota(T.cval[:], [[1, SLOTS]], 0, 0, **fl).then_inc(sem.i_val, 1)
     g.iota(T.cfirst[:], [[SLOTS, 3]], -POOL - 16, 1, **fl).then_inc(sem.i_first, 1)
     g.iota(T.cdmp[:], [[16, SLOTS // 16]], TAB, 1).then_inc(sem.i_dmp, 1)
-    g.iota(T.crow[:], [[0, 1]], 0, 1).then_inc(sem.i_row, 1)
+    g.iota(T.cval[:], [[1, SLOTS]], 0, 0, **fl).then_inc(sem.i_val, 1)
     v.memset(T.nwt[:, 4 * NW:512], 0.0).then_inc(sem.zero, 1)
     v.memset(T.turned[:, 0:32], 0.0).then_inc(sem.k_fill, 1)
     v.memset(T.offr[:], 0).then_inc(sem.k_fill, 1)
+    wait(v, "i_first")
+    v.tensor_scalar(T.cshift[:], T.cfirst[:, 0:1], float(-POOL), 16.0, op.is_lt, op.mult).then_inc(sem.k_shift, 1)
+    wait(v, "i_dmp")
+    v.tensor_copy(T.offp[:], T.cdmp[:]).then_inc(sem.k_idle, 1)
     wait(s, "i_val", "i_first")
     for k in range(3):
         n = min(SLOTS, TAB - SLOTS * k)
         s.activation(T.tab[0:32, SLOTS * k:SLOTS * k + n], T.cval[0:32, 0:n], ActivationFunctionType.Identity,
                      bias=T.cfirst[:, k:k + 1]).then_inc(sem.k_tab, 1)
 
-    groups1 = [far, near + peer] if SPLIT1 else [far + near + peer]
-    picks1 = [runs([T.rank_of(d) for d in ds] + ([rank] if peer[0] in ds else [])) for ds in groups1]
-    v.wait_ge(sem.d_wr, 32)
-    for k in range(4):
-        v.tensor_copy(T.offw[32 * k:32 * k + 32, :], T.wrt[:]).then_inc(sem.offw, 1)
+    groups1 = [far, near + peer + [core]]
+    picks1 = [runs([T.rank_of(d) for d in ds]) for ds in groups1]
     v.wait_ge(sem.d_nw, 16)
     wait(v, "zero")
     v.quantize_mx(T.nwq[:], T.nws[:], T.nwt[:]).then_inc(sem.q_nw, 1)
+    v.wait_ge(sem.d_wr, 64)
+    for k in range(2):
+        v.tensor_copy(T.offw[64 * k:64 * k + 64, :], T.wrt[:]).then_inc(sem.offw, 1)
     for q in (v, s):
-        q.wait_ge(sem.offw, 4)
+        q.wait_ge(sem.offw, 2)
         wait(q, "q_nw")
     for k, ps in enumerate(picks1):
         for a, b in ps:
@@ -204,35 +217,24 @@ def rank_program(g, core, T, topo):
             v.tensor_copy(codes(T.win[:, cols]), codes(T.nwq[:, 0:NW]).indirect(lst)).then_inc(sem["c1_%d" % k], 1)
             s.activation(T.wins[:, cols], T.nws[:, 0:NW].indirect(lst), copy).then_inc(sem["s1_%d" % k], 1)
 
-    for k, name in enumerate(("c1_far", "c1_near")):
-        g.wait_ge(sem["c1_%d" % k], len(picks1[k]))
+    for name, done in (("c1_0", "c1_0"), ("c1_1", None), ("c1_2", "c1_1"), ("c1_3", None), ("s1_0", "s1_0"), ("s1_1", "s1_1")):
+        if done:
+            g.wait_ge(sem[done], len(picks1[int(done[-1])]))
         send(name)
-    if HELP1:
-        for k in range(2):
-            g.wait_ge(sem["s1_%d" % k], len(picks1[k]))
-        send("s1_help")
-        send("s1_rest")
-    else:
-        for k, name in enumerate(("s1_far", "s1_near")):
-            g.wait_ge(sem["s1_%d" % k], len(picks1[k]))
-            send(name)
 
     mine = T.cval[:, CW * rank:CW * rank + CW]
+    s.wait_ge(sem.k_tab, 3)
+    s.activation(mine, mine, ActivationFunctionType.Identity, bias=float(SLOTS)).then_inc(sem.k_val, 1)
     v.wait_ge(sem.d_wp, 32)
     v.tensor_scalar(T.wpa[:], T.wpt[:], 4095, None, op.bitwise_and).then_inc(sem.k_wpa, 1)
-    wait(v, "i_first")
-    v.tensor_scalar(T.cshift[:], T.cfirst[:, 0:1], float(-POOL), 16.0, op.is_lt, op.mult).then_inc(sem.k_shift, 1)
-    wait(v, "i_dmp")
-    v.tensor_copy(T.offp[:], T.cdmp[:]).then_inc(sem.k_idle, 1)
-    wait(v, "k_wpa")
-    v.tensor_tensor(T.wpb[:], T.wpa[:], T.cdmp[0:32, :], op.min).then_inc(sem.k_wpb, 1)
-    v.wait_ge(sem.k_tab, 3)
-    v.tensor_scalar(mine, mine, float(SLOTS), None, op.add).then_inc(sem.k_val, 1)
-    wait(v, "k_wpb", "k_idle", "k_shift")
-    v.tensor_scalar(T.offp[0:32, :], T.wpb[:], T.cshift[:, 0:1], None, op.add).then_inc(sem.k_offp, 1)
     v.wait_ge(sem.d_rd, 32)
     v.wait_ge(sem.k_fill, 2)
+    wait(v, "k_shift")
     v.tensor_scalar(T.offr[0:32, :], T.rdt[:], 16.0, T.cshift[:, 0:1], op.mult, op.add).then_inc(sem.k_offr, 1)
+    wait(v, "k_wpa")
+    v.tensor_tensor(T.wpb[:], T.wpa[:], T.cdmp[0:32, :], op.min).then_inc(sem.k_wpb, 1)
+    wait(v, "k_wpb", "k_idle")
+    v.tensor_scalar(T.offp[0:32, :], T.wpb[:], T.cshift[:, 0:1], None, op.add).then_inc(sem.k_offp, 1)
     wait(v, "k_offp", "k_val")
     v.tensor_copy(T.tab[:, 0:DUMP].indirect(T.offp[:, 0:8]), T.cval[:]).then_inc(sem.k_put, 1)
     wait(v, "k_put")
@@ -264,46 +266,64 @@ def rank_program(g, core, T, topo):
             call = q.activation((T.land2s if core in ds else T.slot2s)[:, cols], T.wins[:, 0:WIDE].indirect(lst), copy)
         call.then_inc(sem[done], 1)
 
+    def by_chip(ds):
+        chips = []
+        for d in ds:
+            if not any(d in c for c in chips):
+                chips.append([x for x in ds if x in topo.cores_of(d)])
+        return chips
+
     half = len(near) // 2
-    ready(v, "c", 0)
-    for ds, done in ((far, "c2_0"), (near[:half], "c2_1"), (near[half:], "c2_1"), (peer, "c2_2"), ([core], "own2_c")):
-        pick(v, ds, True, done)
-    ready(s, "s", 1)
-    for ds, done in ((far, "s2_0"), (near[:half], "s2_1"), (peer, "s2_1"), ([core], "own2_s")):
-        pick(s, ds, False, done)
-    ready(v, "s", 1)
-    pick(v, near[half:], False, "s2_1")
-    for name, done, n in (("c2_far", "c2_0", 1), ("c2_near", "c2_1", 2), ("c2_peer", "c2_2", 1), ("s2_far", "s2_0", 1), ("s2_near", "s2_1", 3)):
-        g.wait_ge(sem[done], n)
-        send(name)
-    g.wait_ge(sem.d_pg, 16)
-    g.partition_broadcast(T.pgb[:], T.pgrow[0:1, :], 128).then_inc(sem.pgb, 1)
-    wait(v, "i_row")
-    v.tensor_scalar(T.crow16[:], T.crow[:], 15, None, op.bitwise_and).then_inc(sem.k_row, 1)
     v.wait_ge(sem.d_qw, 16)
     v.quantize_mx(T.qwq[:], T.qws[:], T.qwt[:]).then_inc(sem.q_qw, 1)
+    ready(v, "c", 0)
+    steps = [n for n in mine_calls if n.startswith("c2")]
+    parts = {name: by_chip([w[0] for w in mine_calls[name]]) for name in steps}
+    for name in steps:
+        for ds in parts[name]:
+            pick(v, ds, True, name)
+    ready(s, "s", 1)
+    every = [ds for name in steps for ds in parts[name]]
+    by_v = [ds for ds in every if ds[0] in near[half:] + peer]
+    ssteps = [n for n in mine_calls if n.startswith("s2")]
+    where = {w[0]: n for n in ssteps for w in mine_calls[n]}
+    where[far[0]] = "s2_0"
+    for ds in every:
+        if ds not in by_v:
+            pick(s, ds, False, where[ds[0]])
+    pick(s, [core], False, "own2_s")
+    ready(v, "s", 1)
+    for ds in by_v:
+        pick(v, ds, False, where[ds[0]])
+    pick(v, [core], True, "own2_c")
+    for name in steps:
+        g.wait_ge(sem[name], len(parts[name]))
+        send(name)
+    g.iota(T.crow[:], [[0, 1]], 0, 1).then_inc(sem.i_row, 1)
+    g.wait_ge(sem.d_pg, 16)
+    g.partition_broadcast(T.pgb[:], T.pgrow[0:1, :], 128).then_inc(sem.pgb, 1)
+    for name in ssteps:
+        g.wait_ge(sem[name], len([ds for ds in every if where[ds[0]] == name]))
+        send(name)
+    wait(v, "i_row")
+    v.tensor_scalar(T.crow16[:], T.crow[:], 15, None, op.bitwise_and).then_inc(sem.k_row, 1)
     wait(v, "k_row")
     v.tensor_copy(T.crowf[:], T.crow16[:]).then_inc(sem.k_rowf, 1)
     wait(v, "pgb", "k_rowf")
     v.tensor_scalar(T.off3[:], T.pgb[:], 16.0, T.crowf[:, 0:1], op.mult, op.add).then_inc(sem.k_off3, 1)
 
-    def quarter(k):
-        return slice(64 * k, 64 * k + 64), T.off3[:, 4 * k:4 * k + 4]
-
+    pieces = [(s, 0, 4, 0), (v, 4, 8, 0), (s, 8, 12, 1), (v, 12, 16, 1)]
     wait(v, "own2_c", "k_off3")
     v.wait_ge(sem.in_c2, arrivals["in_c2"])
-    for k in range(4):
-        cols, lst = quarter(k)
-        v.tensor_copy(codes(T.fin[:, cols]), codes(T.land2[:, 0:N * PAGE]).indirect(lst)).then_inc(sem["fc%d" % (k // 2)], 1)
+    for q, a, b, h in pieces:
+        v.tensor_copy(codes(T.fin[:, 16 * a:16 * b]), codes(T.land2[:, 0:N * PAGE]).indirect(T.off3[:, a:b])).then_inc(sem["fc%d" % h], 1)
     wait(s, "own2_s", "k_off3")
     s.wait_ge(sem.in_s2, arrivals["in_s2"])
     wait(v, "own2_s")
     v.wait_ge(sem.in_s2, arrivals["in_s2"])
-    for h in range(2):
-        cols, lst = quarter(2 * h)
-        s.activation(T.fins[:, cols], T.land2s[:, 0:N * PAGE].indirect(lst), copy).then_inc(sem["fs%d" % h], 1)
-        cols, lst = quarter(2 * h + 1)
-        v.tensor_copy(T.fins[:, cols], T.land2s[:, 0:N * PAGE].indirect(lst)).then_inc(sem["fs%d" % h], 1)
+    for q, a, b, h in pieces:
+        out, src = T.fins[:, 16 * a:16 * b], T.land2s[:, 0:N * PAGE].indirect(T.off3[:, a:b])
+        (q.activation(out, src, copy) if q is s else q.tensor_copy(out, src)).then_inc(sem["fs%d" % h], 1)
     wait(t, "q_qw")
     for h in range(2):
         t.wait_ge(sem["fc%d" % h], 2)
@@ -311,14 +331,13 @@ def rank_program(g, core, T, topo):
         for o in range(O):
             t.matmul_mx(T.acc[:, 512 * (2 * o + h):512 * (2 * o + h) + 128], T.qwq[:, 128 * o:128 * o + 128], T.qws[:, 128 * o:128 * o + 128],
                         T.fin[:, 128 * h:128 * h + 128], T.fins[:, 128 * h:128 * h + 128], True, True).then_inc(sem["m%d%d" % (o, h)], 1)
-    for h in range(2):
-        wait(s, "m0%d" % h)
-        s.activation(T.yt[:, 128 * h:128 * h + 128], T.acc[:, 512 * h:512 * h + 128], copy).then_inc(sem["y0%d" % h], 1)
-        wait(v, "m1%d" % h)
-        v.tensor_copy(T.yt[:, 256 + 128 * h:256 + 128 * h + 128], T.acc[:, 1024 + 512 * h:1024 + 512 * h + 128]).then_inc(sem["y1%d" % h], 1)
-    for q, o, h in ((y, 0, 0), (y, 1, 0), (s, 0, 1), (y, 1, 1)):
-        cols = slice(256 * o + 128 * h, 256 * o + 128 * h + 128)
-        wait(q, "y%d%d" % (o, h))
-        q.dma_start(T.y[:, cols], T.yt[:, cols]).then_inc(sem.d_y, 16)
-    y.wait_ge(sem.d_y, 64)
+    for q, o, h in ((s, 0, 0), (v, 1, 0), (s, 0, 1), (v, 1, 1)):
+        k = 2 * o + h
+        out, src = T.yt[:, 128 * k:128 * k + 128], T.acc[:, 512 * k:512 * k + 128]
+        wait(q, "m%d%d" % (o, h))
+        (q.activation(out, src, copy) if q is s else q.tensor_copy(out, src)).then_inc(sem["y%d%d" % (o, h)], 1)
+    for q, a, b, done in ((y, 0, 128, ["y00"]), (s, 128, 384, ["y10", "y01"]), (y, 384, 512, ["y11"])):
+        wait(q, *done)
+        q.dma_start(T.y[:, a:b], T.yt[:, a:b]).then_inc(sem.d_y, 16)
+    y.wait_ge(sem.d_y, 48)
     g.wait_ge(sem.sent, sent)

from concourse.bass import DstId, RemoteDMATransfer
from concourse.mybir import dt, AluOpType, ActivationFunctionType

N, PG, NW, SP, CW, CP, O = 8, 16, 64, 16, 16, 4, 2
POOL = 16 * PG
PAGE = 16 * CP
SLOTS = N * CW
OUT = POOL + SLOTS
WIDE = OUT + SLOTS
TAB = POOL + 32
DUMP = TAB + 2 * SLOTS + 32
F8 = "float8_e4m3fn_x4"

SPLIT1 = True
QW_LATE = False
RELAY = False

SCRATCH = {
    "nwt": ("sbuf", [128, 512], "bfloat16"),
    "plt": ("sbuf", [128, 4 * POOL], "bfloat16"),
    "qwt": ("sbuf", [128, 512 * O], "bfloat16"),
    "nwq": ("sbuf", [128, 128], F8), "nws": ("sbuf", [128, 128], "uint8"),
    "qwq": ("sbuf", [128, 128 * O], F8), "qws": ("sbuf", [128, 128 * O], "uint8"),
    "win": ("sbuf", [128, WIDE], F8), "wins": ("sbuf", [128, WIDE], "uint8"),
    "hop1s": ("sbuf", [128, 2 * CW], "uint8"),
    "hop2": ("sbuf", [128, 2 * PAGE], F8), "hop2s": ("sbuf", [128, 2 * PAGE], "uint8"),
    "slot2": ("sbuf", [128, N * PAGE], F8), "slot2s": ("sbuf", [128, N * PAGE], "uint8"),
    "land2": ("sbuf", [128, N * PAGE], F8), "land2s": ("sbuf", [128, N * PAGE], "uint8"),
    "fin": ("sbuf", [128, POOL], F8), "fins": ("sbuf", [128, POOL], "uint8"),
    "wrt": ("sbuf", [64, SLOTS // 16], "int32"),
    "wpt": ("sbuf", [32, SLOTS // 16], "int32"),
    "rdt": ("sbuf", [32, N * CP // 16], "int32"),
    "pgrow": ("sbuf", [1, SP], "int32"), "pgb": ("sbuf", [128, SP], "int32"),
    "crow": ("sbuf", [128, 1], "int32"), "crow16": ("sbuf", [128, 1], "int32"), "crowf": ("sbuf", [128, 1], "float32"),
    "cfirst": ("sbuf", [32, 3], "float32"), "cshift": ("sbuf", [32, 1], "float32"),
    "cval": ("sbuf", [128, SLOTS], "bfloat16"),
    "cdmp": ("sbuf", [128, SLOTS // 16], "int32"),
    "wpa": ("sbuf", [32, SLOTS // 16], "int32"), "wpb": ("sbuf", [32, SLOTS // 16], "int32"),
    "tab": ("sbuf", [128, DUMP], "bfloat16"), "turned": ("sbuf", [128, TAB], "bfloat16"),
    "offw": ("sbuf", [128, SLOTS // 16], "uint16"),
    "offp": ("sbuf", [128, SLOTS // 16], "uint16"), "offr": ("sbuf", [128, N * CP // 16], "uint16"),
    "list2": ("sbuf", [128, N * CP], "uint16"), "off3": ("sbuf", [128, SP], "uint16"),
    "acc": ("psum", [128, 512 * 4], "float32"),
    "yt": ("sbuf", [128, 256 * O], "float32"),
}
DMA_SEMS = ["d_nw", "d_wr", "d_pl", "d_wp", "d_rd", "d_pg", "d_qw", "d_y"]
EVENTS = ["zero", "offw", "q_nw", "c1_0", "c1_1", "s1_0", "s1_1", "q_pl", "q_qw",
          "i_row", "i_dmp", "i_val", "i_first", "k_fill", "k_shift", "k_tab", "k_idle", "k_val", "k_row", "k_rowf",
          "k_wpa", "k_wpb", "k_offp", "k_put", "k_turn", "k_offr", "k_look", "k_list2", "pgb", "k_off3",
          "c2_0", "c2_1", "c2_2", "c2_3", "c2_4", "s2_0", "s2_1", "s2_2", "s2_3", "own2_c", "own2_s", "fc0", "fc1", "fs0", "fs1",
          "m00", "m01", "m10", "m11", "y00", "y01", "y10", "y11"]
SEMAPHORES = DMA_SEMS + EVENTS + ["in_c1", "in_s1", "in_c2", "in_s2", "fed1", "fed2", "fed3", "sent"]


def kinds(src, cores, topo):
    peer = [d for d in cores if d != src and d in topo.cores_of(src)]
    off = [d for d in cores if d not in topo.cores_of(src)]
    near = [d for d in off if topo.mates(src, d)] + [d for d in off if topo.same_plane(src, d)]
    return near, [d for d in off if d not in near], peer


def helpers(src, cores, topo):
    far = kinds(src, cores, topo)[1]
    free = [c for c in topo.cores_of(src) if c not in cores and topo.die(c) == topo.die(src)]
    first = [c for c in free if topo.may_write(c, far[0])][0]
    return first, [c for c in free if c != first][0]


def deal(dests, engines):
    n = len(engines) // len(dests)
    return [(d, engines[n * i:n * i + n]) for i, d in enumerate(dests)]


def plan(src, cores, topo):
    near, far, peer = kinds(src, cores, topo)
    mate, plane = near[:len(near) // 2], near[len(near) // 2:]
    e = topo.engines(src, near[0])
    rest = [x for x in topo.engines(src, peer[0]) if x not in e]
    me = cores.index(src)
    to_peer = [(peer[0], rest[0::2])]
    to_near = deal(mate, e[0::2]) + deal(plane[::-1], e[1::2])
    to_far = deal(far, e[0::2] + e[1::2])

    def new(pairs, buf, s):
        return [(d, es, buf, OUT + CW * cores.index(d), buf, POOL + CW * me, CW, s) for d, es in pairs]

    def pages(pairs, a, b, s):
        return [(d, es, a, PAGE * cores.index(d), b, PAGE * me, PAGE, s) for d, es in pairs]

    far, mate, plane = [sorted(ds, key=lambda d: topo.die(d) != topo.die(src)) for ds in (far, mate, plane)]

    def steps(a, b, at=2, inside=rest):
        out = [[(far[1], a), (far[0], b)], [(mate[1], a), (plane[1], b)], [(plane[0], a), (mate[0], b)]]
        out[at] += [(peer[0], inside)]
        return out

    out = {src: [("c1_%d" % k, new(ws, "win", "in_c1")) for k, ws in enumerate(steps(e[0::2], e[1::2], 2, rest[0::2]))]}
    a, b = e[0::2], e[1::2]
    rest = rest[0::2]
    out = {src: [("c1_%d" % k, new(ws, "win", "in_c1")) for k, ws in enumerate(
        [[(far[1], a)], [(far[0], b)], [(plane[1], a), (plane[0], b), (peer[0], rest)], [(mate[1], a), (mate[0], b)]])]}
    out[src] += [("s1_0", new(to_far, "wins", "in_s1")), ("s1_1", new(to_near + [(peer[0], rest)], "wins", "in_s1"))]
    out[src] += [("c2_%d" % k, pages(ws, "slot2", "land2", "in_c2")) for k, ws in enumerate(
        [[(far[1], a)], [(far[0], b)], [(plane[1], a), (mate[1], b)], [(plane[0], a), (mate[0], b), (peer[0], rest)]])]
    out[src] += [("s2_%d" % k, pages(ws, "slot2s", "land2s", "in_s2")) for k, ws in enumerate(
        [[(far[1], b), (far[0], a)], [(plane[1], a), (plane[0], b), (peer[0], rest)], [(mate[1], e)], [(mate[0], e)]])]
    if RELAY:
        h = [c for c in topo.cores_of(mate[0]) if c not in cores and topo.die(c) == topo.die(src)][0]
        out[h] = []
        calls = dict(out[src])
        for name, hop, fed in (("s1_0", "hop1s", "fed1"), ("c2_0", "hop2", "fed2")):
            ws = sorted(calls[name], key=lambda w: w[3])
            calls[name] = [(h, e, ws[0][2], ws[0][3], hop, 0, 2 * ws[0][6], fed)]
            eh = topo.engines(h, far[0])
            out[h].append((fed, [(w[0], eh[i::2], hop, w[6] * i, w[4], w[5], w[6], w[7]) for i, w in enumerate(ws)]))
        out[src] = list(calls.items())
    return out


def runs(ranks):
    out = []
    for r in sorted(ranks):
        if out and out[-1][1] == r:
            out[-1] = (out[-1][0], r + 1)
        else:
            out.append((r, r + 1))
    return out


def rank_program(g, core, T, topo):
    sem = T.sem
    cores = list(T.cores)
    calls, arrivals = {}, {}
    for c in cores:
        calls.update(plan(c, cores, topo))
    if core not in calls:
        return
    for cs in calls.values():
        for name, writes in cs:
            for w in writes:
                if core in (w[0] if isinstance(w[0], tuple) else (w[0],)):
                    arrivals[w[7]] = arrivals.get(w[7], 0) + len(w[1])
    mine_calls = dict(calls[core])

    def send(name):
        tr = []
        for d, es, src, at, dst, to, n, arrive in mine_calls[name]:
            ids = [topo.addr(x, core) for x in (d if isinstance(d, tuple) else (d,))]
            a, b = T[src][:, at:at + n], T[dst][:, to:to + n]
            if SCRATCH[src][2] == F8:
                a, b = a.bitcast(dt.uint8), b.bitcast(dt.uint8)
            tr.append(RemoteDMATransfer(dst_ids=[DstId(rid=rid, pnc=pid) for rid, pid in ids], dma_engine_mask=sum(1 << e for e in es),
                                        remote_sem=sem[arrive], srcs=[a], dsts=[b for x in ids]))
        g.remote_dma_fused(tr, local_sem=sem.sent)

    sent = sum(len(w[1]) for ws in mine_calls.values() for w in ws)
    rank = T.rank_of(core)
    if rank is None:
        for name in mine_calls:
            g.wait_ge(sem[name], arrivals[name])
            send(name)
        g.wait_ge(sem.sent, sent)
        return
    v, s, y, t = g.vector, g.scalar, g.sync, g.tensor
    op = AluOpType
    copy = ActivationFunctionType.Copy
    near, far, peer = kinds(core, cores, topo)

    def wait(q, *names):
        for n in names:
            q.wait_ge(sem[n], 1)

    def codes(view):
        return view.bitcast(dt.uint32)

    y.dma_start(T.nwt[:, 0:4 * NW], T.nw[:]).then_inc(sem.d_nw, 16)
    for k in range(4):
        (s if k < 2 else y).dma_start(T.wrt[16 * k:16 * k + 16, :], T.wr[:]).then_inc(sem.d_wr, 16)
    for k in range(2):
        s.dma_start(T.wpt[16 * k:16 * k + 16, :], T.wp[:]).then_inc(sem.d_wp, 16)
        y.dma_start(T.rdt[16 * k:16 * k + 16, :], T.rd[:]).then_inc(sem.d_rd, 16)
    s.dma_start(T.plt[:], T.pl[:]).then_inc(sem.d_pl, 16)
    y.dma_start(T.qwt[:], T.qw[:]).then_inc(sem.d_qw, 16)
    y.dma_start(T.pgrow[0:1, :], T.pg[:]).then_inc(sem.d_pg, 16)

    fl = dict(allow_small_or_imprecise_dtypes=True)
    g.iota(T.cfirst[:], [[SLOTS, 3]], -POOL - 16, 1, **fl).then_inc(sem.i_first, 1)
    g.iota(T.cdmp[:], [[16, SLOTS // 16]], TAB, 1).then_inc(sem.i_dmp, 1)
    g.iota(T.cval[:], [[1, SLOTS]], 0, 0, **fl).then_inc(sem.i_val, 1)
    v.memset(T.nwt[:, 4 * NW:512], 0.0).then_inc(sem.zero, 1)
    v.memset(T.turned[:, 0:32], 0.0).then_inc(sem.k_fill, 1)
    v.memset(T.offr[:], 0).then_inc(sem.k_fill, 1)
    wait(v, "i_first")
    v.tensor_scalar(T.cshift[:], T.cfirst[:, 0:1], float(-POOL), 16.0, op.is_lt, op.mult).then_inc(sem.k_shift, 1)
    wait(v, "i_dmp")
    v.tensor_copy(T.offp[:], T.cdmp[:]).then_inc(sem.k_idle, 1)
    wait(s, "i_val", "i_first")
    for k in range(3):
        n = min(SLOTS, TAB - SLOTS * k)
        s.activation(T.tab[0:32, SLOTS * k:SLOTS * k + n], T.cval[0:32, 0:n], ActivationFunctionType.Identity,
                     bias=T.cfirst[:, k:k + 1]).then_inc(sem.k_tab, 1)

    groups1 = [far, near + peer + [core]]
    picks1 = [runs([T.rank_of(d) for d in ds]) for ds in groups1]
    v.wait_ge(sem.d_nw, 16)
    wait(v, "zero")
    v.quantize_mx(T.nwq[:], T.nws[:], T.nwt[:]).then_inc(sem.q_nw, 1)
    v.wait_ge(sem.d_wr, 64)
    for k in range(2):
        v.tensor_copy(T.offw[64 * k:64 * k + 64, :], T.wrt[:]).then_inc(sem.offw, 1)
    for q in (v, s):
        q.wait_ge(sem.offw, 2)
        wait(q, "q_nw")
    for k, ps in enumerate(picks1):
        for a, b in ps:
            cols, lst = slice(OUT + CW * a, OUT + CW * b), T.offw[:, a:b]
            v.tensor_copy(codes(T.win[:, cols]), codes(T.nwq[:, 0:NW]).indirect(lst)).then_inc(sem["c1_%d" % k], 1)
            s.activation(T.wins[:, cols], T.nws[:, 0:NW].indirect(lst), copy).then_inc(sem["s1_%d" % k], 1)

    for name, done in (("c1_0", "c1_0"), ("c1_1", None), ("c1_2", "c1_1"), ("c1_3", None), ("s1_0", "s1_0"), ("s1_1", "s1_1")):
        if done:
            g.wait_ge(sem[done], len(picks1[int(done[-1])]))
        send(name)

    mine = T.cval[:, CW * rank:CW * rank + CW]
    s.wait_ge(sem.k_tab, 3)
    s.activation(mine, mine, ActivationFunctionType.Identity, bias=float(SLOTS)).then_inc(sem.k_val, 1)
    v.wait_ge(sem.d_wp, 32)
    v.tensor_scalar(T.wpa[:], T.wpt[:], 4095, None, op.bitwise_and).then_inc(sem.k_wpa, 1)
    v.wait_ge(sem.d_rd, 32)
    v.wait_ge(sem.k_fill, 2)
    wait(v, "k_shift")
    v.tensor_scalar(T.offr[0:32, :], T.rdt[:], 16.0, T.cshift[:, 0:1], op.mult, op.add).then_inc(sem.k_offr, 1)
    wait(v, "k_wpa")
    v.tensor_tensor(T.wpb[:], T.wpa[:], T.cdmp[0:32, :], op.min).then_inc(sem.k_wpb, 1)
    wait(v, "k_wpb", "k_idle")
    v.tensor_scalar(T.offp[0:32, :], T.wpb[:], T.cshift[:, 0:1], None, op.add).then_inc(sem.k_offp, 1)
    wait(v, "k_offp", "k_val")
    v.tensor_copy(T.tab[:, 0:DUMP].indirect(T.offp[:, 0:8]), T.cval[:]).then_inc(sem.k_put, 1)
    wait(v, "k_put")
    v.transpose(T.turned[0:32, :], T.tab[0:32, 0:TAB]).then_inc(sem.k_turn, 1)
    v.wait_ge(sem.d_pl, 16)
    v.quantize_mx(T.win[:, 0:128], T.wins[:, 0:128], T.plt[:, 0:512]).then_inc(sem.q_pl, 1)
    wait(v, "k_turn", "k_offr")
    v.tensor_scalar(T.list2[:], T.turned[:, 0:TAB].indirect(T.offr[:, 0:2]), float(POOL), None, op.add).then_inc(sem.k_look, 1)
    v.quantize_mx(T.win[:, 128:POOL], T.wins[:, 128:POOL], T.plt[:, 512:4 * POOL]).then_inc(sem.q_pl, 1)
    wait(v, "k_look")
    for k in range(1, 4):
        v.tensor_copy(T.list2[32 * k:32 * k + 32, :], T.list2[0:32, :]).then_inc(sem.k_list2, 1)

    def ready(q, kind, n):
        q.wait_ge(sem.k_list2, 3)
        q.wait_ge(sem.q_pl, 2)
        for k, ps in enumerate(picks1):
            q.wait_ge(sem["%s1_%d" % (kind, k)], len(ps))
        q.wait_ge(sem["in_%s1" % kind], arrivals["in_%s1" % kind])

    def pick(q, ds, bits, done):
        (a, b), = runs([T.rank_of(d) for d in ds])
        cols, lst = slice(PAGE * a, PAGE * b), T.list2[:, CP * a:CP * b]
        if bits:
            call = q.tensor_copy(codes((T.land2 if core in ds else T.slot2)[:, cols]), codes(T.win[:, 0:WIDE]).indirect(lst))
        elif q is v:
            call = q.tensor_copy((T.land2s if core in ds else T.slot2s)[:, cols], T.wins[:, 0:WIDE].indirect(lst))
        else:
            call = q.activation((T.land2s if core in ds else T.slot2s)[:, cols], T.wins[:, 0:WIDE].indirect(lst), copy)
        call.then_inc(sem[done], 1)

    def by_chip(ds):
        chips = []
        for d in ds:
            if not any(d in c for c in chips):
                chips.append([x for x in ds if x in topo.cores_of(d)])
        return chips

    half = len(near) // 2
    v.wait_ge(sem.d_qw, 16)
    v.quantize_mx(T.qwq[:], T.qws[:], T.qwt[:]).then_inc(sem.q_qw, 1)
    ready(v, "c", 0)
    steps = [n for n in mine_calls if n.startswith("c2")]
    parts = {name: by_chip([w[0] for w in mine_calls[name]]) for name in steps}
    for name in steps:
        for ds in parts[name]:
            pick(v, ds, True, name)
    ready(s, "s", 1)
    every = [ds for name in steps for ds in parts[name]]
    by_v = [ds for ds in every if ds[0] in near[half:] + peer]
    ssteps = [n for n in mine_calls if n.startswith("s2")]
    where = {w[0]: n for n in ssteps for w in mine_calls[n]}
    where[far[0]] = "s2_0"
    for ds in every:
        if ds not in by_v:
            pick(s, ds, False, where[ds[0]])
    pick(s, [core], False, "own2_s")
    ready(v, "s", 1)
    for ds in by_v:
        pick(v, ds, False, where[ds[0]])
    pick(v, [core], True, "own2_c")
    for name in steps:
        g.wait_ge(sem[name], len(parts[name]))
        send(name)
    g.iota(T.crow[:], [[0, 1]], 0, 1).then_inc(sem.i_row, 1)
    g.wait_ge(sem.d_pg, 16)
    g.partition_broadcast(T.pgb[:], T.pgrow[0:1, :], 128).then_inc(sem.pgb, 1)
    for name in ssteps:
        g.wait_ge(sem[name], len([ds for ds in every if where[ds[0]] == name]))
        send(name)
    wait(v, "i_row")
    v.tensor_scalar(T.crow16[:], T.crow[:], 15, None, op.bitwise_and).then_inc(sem.k_row, 1)
    wait(v, "k_row")
    v.tensor_copy(T.crowf[:], T.crow16[:]).then_inc(sem.k_rowf, 1)
    wait(v, "pgb", "k_rowf")
    v.tensor_scalar(T.off3[:], T.pgb[:], 16.0, T.crowf[:, 0:1], op.mult, op.add).then_inc(sem.k_off3, 1)

    pieces = [(s, 0, 4, 0), (v, 4, 8, 0), (s, 8, 12, 1), (v, 12, 16, 1)]
    wait(v, "own2_c", "k_off3")
    v.wait_ge(sem.in_c2, arrivals["in_c2"])
    for q, a, b, h in pieces:
        v.tensor_copy(codes(T.fin[:, 16 * a:16 * b]), codes(T.land2[:, 0:N * PAGE]).indirect(T.off3[:, a:b])).then_inc(sem["fc%d" % h], 1)
    wait(s, "own2_s", "k_off3")
    s.wait_ge(sem.in_s2, arrivals["in_s2"])
    wait(v, "own2_s")
    v.wait_ge(sem.in_s2, arrivals["in_s2"])
    for q, a, b, h in pieces:
        out, src = T.fins[:, 16 * a:16 * b], T.land2s[:, 0:N * PAGE].indirect(T.off3[:, a:b])
        (q.activation(out, src, copy) if q is s else q.tensor_copy(out, src)).then_inc(sem["fs%d" % h], 1)
    wait(t, "q_qw")
    for h in range(2):
        t.wait_ge(sem["fc%d" % h], 2)
        t.wait_ge(sem["fs%d" % h], 2)
        for o in range(O):
            t.matmul_mx(T.acc[:, 512 * (2 * o + h):512 * (2 * o + h) + 128], T.qwq[:, 128 * o:128 * o + 128], T.qws[:, 128 * o:128 * o + 128],
                        T.fin[:, 128 * h:128 * h + 128], T.fins[:, 128 * h:128 * h + 128], True, True).then_inc(sem["m%d%d" % (o, h)], 1)
    for q, o, h in ((s, 0, 0), (v, 1, 0), (s, 0, 1), (v, 1, 1)):
        k = 2 * o + h
        out, src = T.yt[:, 128 * k:128 * k + 128], T.acc[:, 512 * k:512 * k + 128]
        wait(q, "m%d%d" % (o, h))
        (q.activation(out, src, copy) if q is s else q.tensor_copy(out, src)).then_inc(sem["y%d%d" % (o, h)], 1)
    for q, a, b, done in ((y, 0, 128, ["y00"]), (s, 128, 384, ["y10", "y01"]), (y, 384, 512, ["y11"])):
        wait(q, *done)
        q.dma_start(T.y[:, a:b], T.yt[:, a:b]).then_inc(sem.d_y, 16)
    y.wait_ge(sem.d_y, 48)
    g.wait_ge(sem.sent, sent)
